import numpy as np
import ml_dtypes


def mxq(x, axis, fmt="e4m3"):
    dtype, down = {"e4m3": (ml_dtypes.float8_e4m3fn, 7), "e5m2": (ml_dtypes.float8_e5m2, 14)}[fmt]
    v = np.moveaxis(np.asarray(x, np.float32).astype(ml_dtypes.bfloat16).astype(np.float64), axis, -1)
    blocks = v.reshape(v.shape[:-1] + (-1, 32))
    amax = np.abs(blocks).max(-1, keepdims=True)
    byte = np.maximum(np.where(amax > 0, np.frexp(amax)[1] - 1 + 127, 0) - down, 1)
    scale = np.exp2(byte - 127.0)
    codes = (blocks / scale).astype(np.float32).astype(dtype).astype(np.float64)
    return np.moveaxis((codes * scale).reshape(v.shape), -1, axis)


WIDE = False


def mx_kscale(k):
    if not WIDE:
        return np.ones(k)
    levels = np.array([10, -10, 5, -5, 0])
    if k % 512:
        return np.exp2(np.random.permutation(np.resize(levels, k // 32))).repeat(32)
    a = np.empty((k // 512, 16))
    for p in range(k // 512):
        a[p, :8] = np.random.permutation(np.resize(levels, 8))
        for g in range(8):
            far = levels[np.abs(levels - a[p, g]) >= 10]
            a[p, g + 8] = far[np.random.randint(len(far))]
    return np.exp2(a.ravel()).repeat(32)


def f64(x):
    return np.asarray(x).astype(np.float64)


def striped(idx):
    return np.tile(idx.reshape(-1, 16).T, (8, 1)).astype(np.uint16)


def unstriped(offs):
    return offs[:16].T.reshape(-1).astype(np.int64)


def pack_weight(w):
    k, n = w.shape
    w = f64(np.asarray(w, np.float32).astype(ml_dtypes.bfloat16)).reshape(k // 32, 32, n)
    amax = np.abs(w).max(1)
    byte = np.clip(np.where(amax > 0, np.frexp(amax)[1] - 1 + 127 - 7, 1), 1, 254)
    scaled = (w * np.exp2(127.0 - byte)[:, None, :]).reshape(k, n).astype(np.float32)
    words = np.ascontiguousarray(scaled.reshape(k // 512, 128, 4, n).transpose(0, 1, 3, 2)).astype(ml_dtypes.float8_e4m3fn).view(np.uint8)
    return words, np.ascontiguousarray(byte.astype(np.uint8).reshape(k // 512, 16, n))


def unpack_weight(words, scales):
    g, p, n, _ = words.shape
    vals = np.ascontiguousarray(words).view(ml_dtypes.float8_e4m3fn).astype(np.float64) * np.repeat(np.exp2(scales.astype(np.float64) - 127.0), 8, axis=1)[..., None]
    return vals.transpose(0, 1, 3, 2).reshape(g * 512, n)


K, T, S, V, U = 1024, 2048, 512, 256, 256


def setup_inputs():
    n = np.random.standard_normal
    s = mx_kscale(K)[:, None]
    packed_xT = pack_weight(n((K, T)) * s)
    return {
        "x_words": packed_xT[0],
        "x_scales": packed_xT[1],
        "h0": (n((K, V)) / np.sqrt(K) / s).astype(np.float32),
        "h1": (n((K, V)) / np.sqrt(K) / s).astype(np.float32),
        "h2": (n((K, V)) / np.sqrt(K) / s).astype(np.float32),
        "offs": striped(np.random.permutation(T)[:S]),
        "tree1": striped(np.random.randint(0, S, U)),
        "tree2": striped(np.random.randint(0, S, U)),
        "tree3": striped(np.random.randint(0, S, U)),
    }


def reference(x_words, x_scales, h0, h1, h2, offs, tree1, tree2, tree3):
    h0q = mxq(f64(h0), 0, "e4m3")
    xq = unpack_weight(x_words, x_scales)[:, unstriped(offs)]
    y0 = h0q.T @ xq
    e0 = np.exp(y0)
    s0 = np.log(e0.sum(axis=1, keepdims=True))
    l0 = y0 - s0
    h1q = mxq(f64(h1), 0, "e4m3")
    y1 = h1q.T @ xq
    e1 = np.exp(y1)
    s1 = np.log(e1.sum(axis=1, keepdims=True))
    l1 = y1 - s1
    h2q = mxq(f64(h2), 0, "e4m3")
    y2 = h2q.T @ xq
    e2 = np.exp(y2)
    s2 = np.log(e2.sum(axis=1, keepdims=True))
    l2 = y2 - s2
    return l0[:, unstriped(tree1)] + l1[:, unstriped(tree2)] + l2[:, unstriped(tree3)]

@@ -1,0 +1,195 @@
+import math
+from contextlib import ExitStack
+
+import concourse.mybir as mybir
+
+K, T, S, V, U = 1024, 2048, 512, 256, 256
+HEADS = 3
+FLOPS = 2 * HEADS * K * V * S
+
+F32 = mybir.dt.float32
+BF16 = mybir.dt.bfloat16
+I32 = mybir.dt.int32
+U32 = mybir.dt.uint32
+U16 = mybir.dt.uint16
+U8 = mybir.dt.uint8
+FP8X4 = mybir.dt.float8_e4m3fn_x4
+ACT = mybir.ActivationFunctionType
+ALU = mybir.AluOpType
+
+P = 128
+PACK = 4
+K_PASS = P * PACK
+PASSES = K // K_PASS
+ROW_TILES = V // P
+NODES = 64
+STEP = 0.46
+FIRST = -26.4
+
+
+def tile_picked_ymedu_logs_p_kernel(
+    tc, x_words, x_scales, h0, h1, h2, offs, tree1, tree2, tree3, out
+):
+    nc = tc.nc
+    heads = (h0, h1, h2)
+    trees = (tree1, tree2, tree3)
+    sum_at_one = STEP * sum(math.e ** -(math.e ** (FIRST + STEP * n)) for n in range(NODES))
+
+    with ExitStack() as ctx:
+        keep = ctx.enter_context(tc.tile_pool(name="keep", bufs=1))
+        ring = ctx.enter_context(tc.tile_pool(name="ring", bufs=2))
+        psum = ctx.enter_context(tc.psum_pool(name="psum", bufs=1))
+
+        offsets = keep.tile([P, S // 16], U16, name="offsets")
+        tree_offsets = [keep.tile([P, U // 16], U16, name="tree%d" % i) for i in range(HEADS)]
+        words = [keep.tile([P, T], I32, name="words%d" % g, align_bytes=64) for g in range(PASSES)]
+        scale_rows = keep.tile([P, T], U8, name="scale_rows", align_bytes=64)
+        raw = [[keep.tile([P, PACK, V], F32, name="raw%d_%d" % (i, g), align_bytes=64) for g in range(PASSES)] for i in range(HEADS)]
+
+        def load_h(i, g):
+            rows = heads[i][g * K_PASS : (g + 1) * K_PASS, :]
+            nc.sync.dma_start(out=raw[i][g][:], in_=rows.rearrange("(p j) t -> p j t", j=PACK))
+
+        def load_words(g):
+            nc.sync.dma_start(out=words[g][:], in_=x_words[g].rearrange("p n b -> p (n b)").bitcast(I32))
+
+        nc.vector.memset(scale_rows[:].bitcast(I32), 0)
+        nc.sync.dma_start(offsets[:], offs)
+        load_words(0)
+        for q in range(4):
+            nc.sync.dma_start(
+                out=scale_rows[32 * q : 32 * q + 4 * PASSES, :].bitcast(I32),
+                in_=x_scales[:, 4 * q : 4 * q + 4, :].bitcast(I32),
+            )
+        load_h(0, 0)
+        load_words(1)
+        load_h(0, 1)
+        load_h(1, 0)
+        for i in range(HEADS):
+            nc.sync.dma_start(tree_offsets[i][:], trees[i])
+        load_h(1, 1)
+        load_h(2, 0)
+        load_h(2, 1)
+
+        count = keep.tile([P, NODES], I32, name="count")
+        nc.gpsimd.iota(count[:], [[1, NODES]], base=0, channel_multiplier=0)
+        count_f = keep.tile([P, NODES], F32, name="count_f")
+        nc.vector.tensor_copy(count_f[:], count[:])
+        exponent = keep.tile([P, NODES], F32, name="exponent")
+        nc.vector.tensor_scalar(exponent[:], count_f[:], STEP, FIRST, ALU.mult, ALU.add)
+        nodes = keep.tile([P, NODES], F32, name="nodes")
+        nc.scalar.activation(nodes[:], exponent[:], ACT.Exp)
+        neg_nodes = keep.tile([P, NODES], F32, name="neg_nodes")
+        nc.vector.tensor_scalar(neg_nodes[:], nodes[:], -1.0, None, ALU.mult)
+
+        picked_words = [keep.tile([P, S], U32, name="picked_words%d" % g, align_bytes=64) for g in range(PASSES)]
+        picked_scales = keep.tile([P, S], U8, name="picked_scales", align_bytes=64)
+        codes = [[keep.tile([P, V], U32, name="codes%d_%d" % (i, g), align_bytes=64) for g in range(PASSES)] for i in range(HEADS)]
+        planes = [[keep.tile([P, V], U8, name="planes%d_%d" % (i, g), align_bytes=64) for g in range(PASSES)] for i in range(HEADS)]
+        grouped = [[keep.tile([P, V * PACK], BF16, name="grouped%d_%d" % (i, g), align_bytes=64) for g in range(PASSES)] for i in range(HEADS)]
+
+        def gather_words(g):
+            nc.vector.tensor_copy(picked_words[g][:], words[g][:].bitcast(U32).indirect(offsets[:]))
+
+        def interleave(i, g, copy, lo=0, hi=V):
+            copy(
+                grouped[i][g][:, PACK * lo : PACK * hi].rearrange("p (c n j) -> p c j n", n=4, j=PACK),
+                raw[i][g][:, :, lo:hi].rearrange("p j (c n) -> p c j n", n=4),
+            )
+
+        def quantize(i, g, lo=0, hi=V):
+            nc.vector.quantize_mx(
+                out=codes[i][g][:, lo:hi].bitcast(FP8X4),
+                scales=planes[i][g][:, lo:hi],
+                in_=grouped[i][g][:, PACK * lo : PACK * hi],
+            )
+
+        banks = {}
+        stats = {}
+        logp = {}
+        total = {}
+
+        def multiply(i, m, g):
+            if g == 0:
+                banks[i, m] = psum.tile([P, S], F32, name="bank%d_%d" % (i, m))
+            cols = slice(m * P, (m + 1) * P)
+            nc.tensor.matmul_mx(
+                out=banks[i, m][:],
+                lhsT=codes[i][g][:, cols].bitcast(FP8X4),
+                lhsT_scale=planes[i][g][:, cols],
+                rhs=picked_words[g][:].bitcast(FP8X4),
+                rhs_scale=picked_scales[4 * g : P, :],
+                start=(g == 0),
+                stop=(g == PASSES - 1),
+            )
+
+        def row_max(i, m):
+            stats[i, m] = keep.tile([P, 8], F32, name="stats%d_%d" % (i, m))
+            nc.vector.tensor_reduce(stats[i, m][:, 0:1], banks[i, m][:], mybir.AxisListType.X, ALU.max, negate=True)
+
+        def log_softmax(i, m):
+            st = stats[i, m]
+            neg_max, z, shift, a, bias = (st[:, c : c + 1] for c in range(5))
+            exps = ring.tile([P, S], F32, name="exps")
+            nc.scalar.activation(exps[:], banks[i, m][:], ACT.Exp, bias=neg_max, accum_out=z)
+            nc.scalar.activation(shift, neg_max, ACT.Identity, bias=-sum_at_one)
+            terms = ring.tile([P, NODES], F32, name="terms")
+            nc.scalar.activation(terms[:], neg_nodes[:], ACT.Exp, scale=z, accum_out=a)
+            nc.scalar.activation(bias, a, ACT.Identity, scale=STEP, bias=shift)
+            logp[i, m] = keep.tile([P, S], F32, name="logp%d_%d" % (i, m))
+            nc.scalar.activation(logp[i, m][:], banks[i, m][:], ACT.Identity, bias=bias)
+
+        def fetch(i, m):
+            acc = keep.tile([P, U], F32, name="total%d_%d" % (i, m))
+            looked_up = logp[i, m][:].indirect(tree_offsets[i][:])
+            if i == 0:
+                nc.vector.tensor_copy(acc[:], looked_up)
+            else:
+                nc.vector.tensor_tensor(acc[:], looked_up, total[m][:], ALU.add)
+            total[m] = acc
+            if i == HEADS - 1:
+                nc.sync.dma_start(out=out[m * P : (m + 1) * P, :], in_=acc[:])
+
+        gather_words(0)
+        nc.vector.tensor_copy(picked_scales[:], scale_rows[:].indirect(offsets[:]))
+        interleave(0, 0, nc.scalar.copy)
+        quantize(0, 0)
+        gather_words(1)
+        for m in range(ROW_TILES):
+            multiply(0, m, 0)
+        interleave(0, 1, nc.vector.tensor_copy, 0, P)
+        interleave(0, 1, nc.scalar.copy, P, V)
+        quantize(0, 1, 0, P)
+        multiply(0, 0, 1)
+        quantize(0, 1, P, V)
+        multiply(0, 1, 1)
+        interleave(1, 0, nc.scalar.copy)
+        row_max(0, 0)
+        log_softmax(0, 0)
+        quantize(1, 0)
+        multiply(1, 0, 0)
+        interleave(1, 1, nc.vector.tensor_copy)
+        row_max(0, 1)
+        log_softmax(0, 1)
+        quantize(1, 1)
+        multiply(1, 0, 1)
+        multiply(1, 1, 0)
+        multiply(1, 1, 1)
+        interleave(2, 0, nc.vector.tensor_copy)
+        row_max(1, 0)
+        log_softmax(1, 0)
+        quantize(2, 0)
+        interleave(2, 1, nc.vector.tensor_copy)
+        row_max(1, 1)
+        log_softmax(1, 1)
+        quantize(2, 1)
+        for m in range(ROW_TILES):
+            for g in range(PASSES):
+                multiply(2, m, g)
+        row_max(2, 0)
+        log_softmax(2, 0)
+        row_max(2, 1)
+        log_softmax(2, 1)
+        for i in range(HEADS):
+            for m in range(ROW_TILES):
+                fetch(i, m)

@@ -22,9 +22,17 @@ PACK = 4
 K_PASS = P * PACK
 PASSES = K // K_PASS
 ROW_TILES = V // P
+QUADRANTS = 4
+SCALE_ROWS = 4
+LIST_GROUP = 16
+RUN = 4
+LAST_HEAD = HEADS - 1
+
 NODES = 64
 STEP = 0.46
 FIRST = -26.4
+
+NEG_MAX, SUM, SHIFT, QUAD, BIAS = range(5)
 
 
 def tile_picked_ymedu_logs_p_kernel(
@@ -33,68 +41,69 @@ def tile_picked_ymedu_logs_p_kernel(
     nc = tc.nc
     heads = (h0, h1, h2)
     trees = (tree1, tree2, tree3)
-    sum_at_one = STEP * sum(math.e ** -(math.e ** (FIRST + STEP * n)) for n in range(NODES))
+    rule_at_one = STEP * sum(math.e ** -(math.e ** (FIRST + STEP * n)) for n in range(NODES))
 
     with ExitStack() as ctx:
         keep = ctx.enter_context(tc.tile_pool(name="keep", bufs=1))
         ring = ctx.enter_context(tc.tile_pool(name="ring", bufs=2))
         psum = ctx.enter_context(tc.psum_pool(name="psum", bufs=1))
 
-        offsets = keep.tile([P, S // 16], U16, name="offsets")
-        tree_offsets = [keep.tile([P, U // 16], U16, name="tree%d" % i) for i in range(HEADS)]
+        def per_head_and_pass(label, shape, dtype):
+            return [
+                [keep.tile(shape, dtype, name="%s%d_%d" % (label, i, g), align_bytes=64) for g in range(PASSES)]
+                for i in range(HEADS)
+            ]
+
+        offsets = keep.tile([P, S // LIST_GROUP], U16, name="offsets")
+        tree_offsets = [keep.tile([P, U // LIST_GROUP], U16, name="tree%d" % i) for i in range(HEADS)]
         words = [keep.tile([P, T], I32, name="words%d" % g, align_bytes=64) for g in range(PASSES)]
         scale_rows = keep.tile([P, T], U8, name="scale_rows", align_bytes=64)
-        raw = [[keep.tile([P, PACK, V], F32, name="raw%d_%d" % (i, g), align_bytes=64) for g in range(PASSES)] for i in range(HEADS)]
+        raw = per_head_and_pass("raw", [P, PACK, V], F32)
 
-        def load_h(i, g):
+        def load_head(i, g):
             rows = heads[i][g * K_PASS : (g + 1) * K_PASS, :]
             nc.sync.dma_start(out=raw[i][g][:], in_=rows.rearrange("(p j) t -> p j t", j=PACK))
 
         def load_words(g):
             nc.sync.dma_start(out=words[g][:], in_=x_words[g].rearrange("p n b -> p (n b)").bitcast(I32))
 
-        nc.vector.memset(scale_rows[:].bitcast(I32), 0)
+        nc.gpsimd.memset(scale_rows[:].bitcast(I32), 0)
         nc.sync.dma_start(offsets[:], offs)
         load_words(0)
-        for q in range(4):
+        for q in range(QUADRANTS):
             nc.sync.dma_start(
-                out=scale_rows[32 * q : 32 * q + 4 * PASSES, :].bitcast(I32),
-                in_=x_scales[:, 4 * q : 4 * q + 4, :].bitcast(I32),
+                out=scale_rows[32 * q : 32 * q + SCALE_ROWS * PASSES, :].bitcast(I32),
+                in_=x_scales[:, SCALE_ROWS * q : SCALE_ROWS * (q + 1), :].bitcast(I32),
             )
-        load_h(0, 0)
+        load_head(0, 0)
         load_words(1)
-        load_h(0, 1)
-        load_h(1, 0)
+        load_head(0, 1)
+        for i in range(1, HEADS):
+            for g in range(PASSES):
+                load_head(i, g)
         for i in range(HEADS):
             nc.sync.dma_start(tree_offsets[i][:], trees[i])
-        load_h(1, 1)
-        load_h(2, 0)
-        load_h(2, 1)
 
-        count = keep.tile([P, NODES], I32, name="count")
-        nc.gpsimd.iota(count[:], [[1, NODES]], base=0, channel_multiplier=0)
-        count_f = keep.tile([P, NODES], F32, name="count_f")
-        nc.vector.tensor_copy(count_f[:], count[:])
-        exponent = keep.tile([P, NODES], F32, name="exponent")
-        nc.vector.tensor_scalar(exponent[:], count_f[:], STEP, FIRST, ALU.mult, ALU.add)
+        count = keep.tile([P, NODES], F32, name="count")
+        nc.gpsimd.iota(count[:], [[1, NODES]], base=0, channel_multiplier=0, allow_small_or_imprecise_dtypes=True)
         nodes = keep.tile([P, NODES], F32, name="nodes")
-        nc.scalar.activation(nodes[:], exponent[:], ACT.Exp)
+        nc.scalar.activation(nodes[:], count[:], ACT.Exp, scale=STEP, bias=FIRST)
         neg_nodes = keep.tile([P, NODES], F32, name="neg_nodes")
-        nc.vector.tensor_scalar(neg_nodes[:], nodes[:], -1.0, None, ALU.mult)
+        nc.scalar.activation(neg_nodes[:], nodes[:], ACT.Copy, scale=-1.0)
 
         picked_words = [keep.tile([P, S], U32, name="picked_words%d" % g, align_bytes=64) for g in range(PASSES)]
         picked_scales = keep.tile([P, S], U8, name="picked_scales", align_bytes=64)
-        codes = [[keep.tile([P, V], U32, name="codes%d_%d" % (i, g), align_bytes=64) for g in range(PASSES)] for i in range(HEADS)]
-        planes = [[keep.tile([P, V], U8, name="planes%d_%d" % (i, g), align_bytes=64) for g in range(PASSES)] for i in range(HEADS)]
-        grouped = [[keep.tile([P, V * PACK], BF16, name="grouped%d_%d" % (i, g), align_bytes=64) for g in range(PASSES)] for i in range(HEADS)]
+        codes = per_head_and_pass("codes", [P, V], U32)
+        planes = per_head_and_pass("planes", [P, V], U8)
+        grouped = per_head_and_pass("grouped", [P, V * PACK], BF16)
 
         def gather_words(g):
             nc.vector.tensor_copy(picked_words[g][:], words[g][:].bitcast(U32).indirect(offsets[:]))
 
         def interleave(i, g, copy, lo=0, hi=V):
             copy(
-                grouped[i][g][:, PACK * lo : PACK * hi].rearrange("p (c n j) -> p c j n", n=4, j=PACK),
-                raw[i][g][:, :, lo:hi].rearrange("p j (c n) -> p c j n", n=4),
+                grouped[i][g][:, PACK * lo : PACK * hi].rearrange("p (c n j) -> p c j n", n=RUN, j=PACK),
+                raw[i][g][:, :, lo:hi].rearrange("p j (c n) -> p c j n", n=RUN),
             )
 
         def quantize(i, g, lo=0, hi=V):
@@ -118,78 +127,106 @@ def tile_picked_ymedu_logs_p_kernel(
                 lhsT=codes[i][g][:, cols].bitcast(FP8X4),
                 lhsT_scale=planes[i][g][:, cols],
                 rhs=picked_words[g][:].bitcast(FP8X4),
-                rhs_scale=picked_scales[4 * g : P, :],
+                rhs_scale=picked_scales[SCALE_ROWS * g : P, :],
                 start=(g == 0),
                 stop=(g == PASSES - 1),
             )
 
+        def column(i, m, c):
+            return stats[i, m][:, c : c + 1]
+
         def row_max(i, m):
             stats[i, m] = keep.tile([P, 8], F32, name="stats%d_%d" % (i, m))
-            nc.vector.tensor_reduce(stats[i, m][:, 0:1], banks[i, m][:], mybir.AxisListType.X, ALU.max, negate=True)
+            nc.vector.tensor_reduce(column(i, m, NEG_MAX), banks[i, m][:], mybir.AxisListType.X, ALU.max, negate=True)
 
-        def log_softmax(i, m):
-            st = stats[i, m]
-            neg_max, z, shift, a, bias = (st[:, c : c + 1] for c in range(5))
+        def sum_of_exps(i, m):
             exps = ring.tile([P, S], F32, name="exps")
-            nc.scalar.activation(exps[:], banks[i, m][:], ACT.Exp, bias=neg_max, accum_out=z)
-            nc.scalar.activation(shift, neg_max, ACT.Identity, bias=-sum_at_one)
-            terms = ring.tile([P, NODES], F32, name="terms")
-            nc.scalar.activation(terms[:], neg_nodes[:], ACT.Exp, scale=z, accum_out=a)
-            nc.scalar.activation(bias, a, ACT.Identity, scale=STEP, bias=shift)
-            logp[i, m] = keep.tile([P, S], F32, name="logp%d_%d" % (i, m))
-            nc.scalar.activation(logp[i, m][:], banks[i, m][:], ACT.Identity, bias=bias)
+            nc.scalar.activation(
+                exps[:], banks[i, m][:], ACT.Exp, bias=column(i, m, NEG_MAX), accum_out=column(i, m, SUM)
+            )
+            nc.scalar.activation(column(i, m, SHIFT), column(i, m, NEG_MAX), ACT.Identity, bias=-rule_at_one)
 
-        def fetch(i, m):
-            acc = keep.tile([P, U], F32, name="total%d_%d" % (i, m))
-            looked_up = logp[i, m][:].indirect(tree_offsets[i][:])
-            if i == 0:
-                nc.vector.tensor_copy(acc[:], looked_up)
-            else:
-                nc.vector.tensor_tensor(acc[:], looked_up, total[m][:], ALU.add)
+        def quadrature(i, m):
+            terms = ring.tile([P, NODES], F32, name="terms")
+            nc.scalar.activation(
+                terms[:], neg_nodes[:], ACT.Exp, scale=column(i, m, SUM), accum_out=column(i, m, QUAD)
+            )
+
+        def row_bias(i, m):
+            nc.scalar.activation(
+                column(i, m, BIAS), column(i, m, QUAD), ACT.Identity, scale=STEP, bias=column(i, m, SHIFT)
+            )
+
+        def log_probabilities(i, m):
+            logp[i, m] = keep.tile([P, S], F32, name="logp%d_%d" % (i, m))
+            nc.scalar.activation(logp[i, m][:], banks[i, m][:], ACT.Identity, bias=column(i, m, BIAS))
+
+        last_operand = "%d_%d" % (LAST_HEAD, PASSES - 1)
+        reused = {(0, 0): "grouped" + last_operand, (0, 1): "planes" + last_operand, (1, 0): "codes" + last_operand}
+
+        def fetch(i, m, pieces):
+            width = U // pieces
+            for c in range(pieces):
+                label = "total%d_%d_%d" % (i, m, c)
+                acc = keep.tile([P, width], F32, name=label, tag=reused.get((i, m), label), align_bytes=64)
+                cols = slice(c * width, (c + 1) * width)
+                entries = tree_offsets[i][:, c * width // LIST_GROUP : (c + 1) * width // LIST_GROUP]
+                if i == 0:
+                    nc.vector.tensor_copy(acc[:], logp[i, m][:].indirect(entries))
+                else:
+                    nc.vector.tensor_tensor(acc[:], logp[i, m][:].indirect(entries), total[m][:, cols], ALU.add)
+                if i == LAST_HEAD:
+                    nc.sync.dma_start(out=out[m * P : (m + 1) * P, cols], in_=acc[:])
             total[m] = acc
-            if i == HEADS - 1:
-                nc.sync.dma_start(out=out[m * P : (m + 1) * P, :], in_=acc[:])
 
         gather_words(0)
         nc.vector.tensor_copy(picked_scales[:], scale_rows[:].indirect(offsets[:]))
-        interleave(0, 0, nc.scalar.copy)
+        interleave(0, 0, nc.vector.tensor_copy)
         quantize(0, 0)
         gather_words(1)
         for m in range(ROW_TILES):
             multiply(0, m, 0)
         interleave(0, 1, nc.vector.tensor_copy, 0, P)
         interleave(0, 1, nc.scalar.copy, P, V)
-        quantize(0, 1, 0, P)
-        multiply(0, 0, 1)
-        quantize(0, 1, P, V)
-        multiply(0, 1, 1)
+        for m in range(ROW_TILES):
+            quantize(0, 1, m * P, (m + 1) * P)
+            multiply(0, m, 1)
+
         interleave(1, 0, nc.scalar.copy)
         row_max(0, 0)
-        log_softmax(0, 0)
-        quantize(1, 0)
-        multiply(1, 0, 0)
-        interleave(1, 1, nc.vector.tensor_copy)
         row_max(0, 1)
-        log_softmax(0, 1)
+        sum_of_exps(0, 0)
+        quantize(1, 0)
+        interleave(1, 1, nc.scalar.copy, 0, P)
+        interleave(1, 1, nc.vector.tensor_copy, P, V)
         quantize(1, 1)
-        multiply(1, 0, 1)
-        multiply(1, 1, 0)
-        multiply(1, 1, 1)
-        interleave(2, 0, nc.vector.tensor_copy)
-        row_max(1, 0)
-        log_softmax(1, 0)
-        quantize(2, 0)
-        interleave(2, 1, nc.vector.tensor_copy)
-        row_max(1, 1)
-        log_softmax(1, 1)
-        quantize(2, 1)
-        for m in range(ROW_TILES):
-            for g in range(PASSES):
+        for g in range(PASSES):
+            for m in range(ROW_TILES):
+                multiply(1, m, g)
+
+        for g in range(PASSES):
+            for m in range(ROW_TILES):
+                interleave(2, g, nc.vector.tensor_copy, m * P, (m + 1) * P)
+            for m in range(ROW_TILES):
+                quantize(2, g, m * P, (m + 1) * P)
+            row_max(1, g)
+        for g in range(PASSES):
+            for m in range(ROW_TILES):
                 multiply(2, m, g)
         row_max(2, 0)
-        log_softmax(2, 0)
         row_max(2, 1)
-        log_softmax(2, 1)
+
+        for i in range(HEADS):
+            quadrature(i, 0)
+            sum_of_exps(i, 1)
+            row_bias(i, 0)
+            quadrature(i, 1)
+            log_probabilities(i, 0)
+            row_bias(i, 1)
+            if i < LAST_HEAD:
+                sum_of_exps(i + 1, 0)
+            log_probabilities(i, 1)
+
         for i in range(HEADS):
             for m in range(ROW_TILES):
-                fetch(i, m)
+                fetch(i, m, 2 if (i, m) == (LAST_HEAD, ROW_TILES - 1) else 1)

@@ -45,7 +45,7 @@ def tile_picked_ymedu_logs_p_kernel(
 
     with ExitStack() as ctx:
         keep = ctx.enter_context(tc.tile_pool(name="keep", bufs=1))
-        ring = ctx.enter_context(tc.tile_pool(name="ring", bufs=2))
+        staged = ctx.enter_context(tc.tile_pool(name="staged", bufs=1))
         psum = ctx.enter_context(tc.psum_pool(name="psum", bufs=1))
 
         def per_head_and_pass(label, shape, dtype):
@@ -57,8 +57,22 @@ def tile_picked_ymedu_logs_p_kernel(
         offsets = keep.tile([P, S // LIST_GROUP], U16, name="offsets")
         tree_offsets = [keep.tile([P, U // LIST_GROUP], U16, name="tree%d" % i) for i in range(HEADS)]
         words = [keep.tile([P, T], I32, name="words%d" % g, align_bytes=64) for g in range(PASSES)]
-        scale_rows = keep.tile([P, T], U8, name="scale_rows", align_bytes=64)
-        raw = per_head_and_pass("raw", [P, PACK, V], F32)
+
+        def staged_tiles(label, shape, dtype):
+            return [
+                [
+                    staged.tile(shape, dtype, name="%s%d_%d" % (label, i, g), offset=place[label, i, g], align_bytes=64)
+                    for g in range(PASSES)
+                ]
+                for i in range(HEADS)
+            ]
+
+        place = {}
+        for i in range(HEADS):
+            for g in range(PASSES):
+                place["raw", i, g] = (PASSES * i + g) * 6144
+                place["grouped", i, g] = place["raw", i, g] + 4096
+        raw = staged_tiles("raw", [P, PACK, V], F32)
 
         def load_head(i, g):
             rows = heads[i][g * K_PASS : (g + 1) * K_PASS, :]
@@ -67,7 +81,9 @@ def tile_picked_ymedu_logs_p_kernel(
         def load_words(g):
             nc.sync.dma_start(out=words[g][:], in_=x_words[g].rearrange("p n b -> p (n b)").bitcast(I32))
 
-        nc.gpsimd.memset(scale_rows[:].bitcast(I32), 0)
+        scale_rows = keep.tile([P, T], U8, name="scale_rows", align_bytes=64)
+        picked_scales = keep.tile([P, S], U8, name="picked_scales", align_bytes=64)
+        nc.vector.memset(scale_rows[:].bitcast(I32), 0)
         nc.sync.dma_start(offsets[:], offs)
         load_words(0)
         for q in range(QUADRANTS):
@@ -75,14 +91,13 @@ def tile_picked_ymedu_logs_p_kernel(
                 out=scale_rows[32 * q : 32 * q + SCALE_ROWS * PASSES, :].bitcast(I32),
                 in_=x_scales[:, SCALE_ROWS * q : SCALE_ROWS * (q + 1), :].bitcast(I32),
             )
-        load_head(0, 0)
         load_words(1)
-        load_head(0, 1)
-        for i in range(1, HEADS):
+        for i in range(HEADS):
             for g in range(PASSES):
                 load_head(i, g)
         for i in range(HEADS):
             nc.sync.dma_start(tree_offsets[i][:], trees[i])
+
 
         count = keep.tile([P, NODES], F32, name="count")
         nc.gpsimd.iota(count[:], [[1, NODES]], base=0, channel_multiplier=0, allow_small_or_imprecise_dtypes=True)
@@ -92,10 +107,14 @@ def tile_picked_ymedu_logs_p_kernel(
         nc.scalar.activation(neg_nodes[:], nodes[:], ACT.Copy, scale=-1.0)
 
         picked_words = [keep.tile([P, S], U32, name="picked_words%d" % g, align_bytes=64) for g in range(PASSES)]
-        picked_scales = keep.tile([P, S], U8, name="picked_scales", align_bytes=64)
-        codes = per_head_and_pass("codes", [P, V], U32)
+        codes = [
+            [keep.tile([P, V], U32, name="codes%d_%d" % (i, g), align_bytes=64) if (i, g) != (2, 0) else None for g in range(PASSES)]
+            for i in range(HEADS)
+        ]
         planes = per_head_and_pass("planes", [P, V], U8)
-        grouped = per_head_and_pass("grouped", [P, V * PACK], BF16)
+        grouped = staged_tiles("grouped", [P, V * PACK], BF16)
+
+        codes[2][0] = staged.tile([P, V], U32, name="held_codes", offset=place["raw", 2, 1] + 2048 + 1024, align_bytes=64)
 
         def gather_words(g):
             nc.vector.tensor_copy(picked_words[g][:], words[g][:].bitcast(U32).indirect(offsets[:]))
@@ -115,11 +134,13 @@ def tile_picked_ymedu_logs_p_kernel(
 
         banks = {}
         stats = {}
+        negated = {}
         logp = {}
         total = {}
 
         def multiply(i, m, g):
-            if g == 0:
+            first = (i, m) not in banks
+            if first:
                 banks[i, m] = psum.tile([P, S], F32, name="bank%d_%d" % (i, m))
             cols = slice(m * P, (m + 1) * P)
             nc.tensor.matmul_mx(
@@ -128,47 +149,94 @@ def tile_picked_ymedu_logs_p_kernel(
                 lhsT_scale=planes[i][g][:, cols],
                 rhs=picked_words[g][:].bitcast(FP8X4),
                 rhs_scale=picked_scales[SCALE_ROWS * g : P, :],
-                start=(g == 0),
-                stop=(g == PASSES - 1),
+                start=first,
+                stop=not first,
             )
 
+        held = {
+            "stats0_0": ("raw", 1, 0, 0),
+            "exps0_0": ("raw", 1, 1, 0),
+            "terms0_0": ("grouped", 2, 0, 0),
+            "exps0_1": ("raw", 2, 0, 0),
+            "stats1_0": ("raw", 2, 1, 2048),
+            "logp0_0": ("raw", 2, 1, 0),
+            "stats1_1": ("grouped", 2, 1, 0),
+            "total0_0_0": ("grouped", 2, 1, 512),
+        }
+
+        def new_tile(shape, label):
+            if label in held:
+                kind, i, g, within = held[label]
+                return staged.tile(shape, F32, name=label, offset=place[kind, i, g] + within, align_bytes=64)
+            return keep.tile(shape, F32, name=label, align_bytes=64)
+
         def column(i, m, c):
-            return stats[i, m][:, c : c + 1]
+            return stats[i, m][:, 8 * c : 8 * c + 1]
 
         def row_max(i, m):
-            stats[i, m] = keep.tile([P, 8], F32, name="stats%d_%d" % (i, m))
+            label = "stats%d_%d" % (i, m)
+            stats[i, m] = new_tile([P, 40], label)
             nc.vector.tensor_reduce(column(i, m, NEG_MAX), banks[i, m][:], mybir.AxisListType.X, ALU.max, negate=True)
 
+        def row_max_and_copy(i, m):
+            label = "stats%d_%d" % (i, m)
+            stats[i, m] = new_tile([P, 40], label)
+            negated[i, m] = keep.tile([P, S], F32, name="negated%d_%d" % (i, m))
+            nc.vector.tensor_scalar(
+                negated[i, m][:], banks[i, m][:], -1.0, None, ALU.mult, ALU.min, accum_out=column(i, m, NEG_MAX)
+            )
+
         def sum_of_exps(i, m):
-            exps = ring.tile([P, S], F32, name="exps")
+            label = "exps%d_%d" % (i, m)
+            exps = new_tile([P, S], label)
             nc.scalar.activation(
                 exps[:], banks[i, m][:], ACT.Exp, bias=column(i, m, NEG_MAX), accum_out=column(i, m, SUM)
             )
+
+        def shift(i, m):
             nc.scalar.activation(column(i, m, SHIFT), column(i, m, NEG_MAX), ACT.Identity, bias=-rule_at_one)
 
         def quadrature(i, m):
-            terms = ring.tile([P, NODES], F32, name="terms")
+            label = "terms%d_%d" % (i, m)
+            terms = new_tile([P, NODES], label)
             nc.scalar.activation(
-                terms[:], neg_nodes[:], ACT.Exp, scale=column(i, m, SUM), accum_out=column(i, m, QUAD)
+                terms[:],
+                neg_nodes[:],
+                ACT.Exp,
+                scale=column(i, m, SUM),
+                bias=math.log10(STEP) / math.log10(math.e),
+                accum_out=column(i, m, QUAD),
             )
 
         def row_bias(i, m):
-            nc.scalar.activation(
-                column(i, m, BIAS), column(i, m, QUAD), ACT.Identity, scale=STEP, bias=column(i, m, SHIFT)
+            nc.scalar.activation(column(i, m, BIAS), column(i, m, QUAD), ACT.Identity, bias=column(i, m, SHIFT))
+
+        def row_bias_on(engine, i, m):
+            engine.tensor_scalar(
+                column(i, m, BIAS), column(i, m, QUAD), column(i, m, NEG_MAX), -rule_at_one, ALU.add, ALU.add
             )
 
-        def log_probabilities(i, m):
-            logp[i, m] = keep.tile([P, S], F32, name="logp%d_%d" % (i, m))
-            nc.scalar.activation(logp[i, m][:], banks[i, m][:], ACT.Identity, bias=column(i, m, BIAS))
+        def new_logp(i, m):
+            label = "logp%d_%d" % (i, m)
+            logp[i, m] = new_tile([P, S], label)
+            return logp[i, m][:]
 
-        last_operand = "%d_%d" % (LAST_HEAD, PASSES - 1)
-        reused = {(0, 0): "grouped" + last_operand, (0, 1): "planes" + last_operand, (1, 0): "codes" + last_operand}
+        def logp_on_scalar(i, m):
+            nc.scalar.activation(new_logp(i, m), banks[i, m][:], ACT.Identity, bias=column(i, m, BIAS))
 
-        def fetch(i, m, pieces):
+        def logp_from_copy(engine, i, m):
+            engine.tensor_scalar(new_logp(i, m), negated[i, m][:], -1.0, column(i, m, BIAS), ALU.mult, ALU.add)
+
+        def logp_from_bank(i, m):
+            nc.vector.tensor_scalar(
+                new_logp(i, m), banks[i, m][:], column(i, m, SHIFT), column(i, m, QUAD), ALU.add, ALU.add
+            )
+
+        def fetch(i, m, pieces=1):
             width = U // pieces
             for c in range(pieces):
                 label = "total%d_%d_%d" % (i, m, c)
-                acc = keep.tile([P, width], F32, name=label, tag=reused.get((i, m), label), align_bytes=64)
+                acc = new_tile([P, width], label)
                 cols = slice(c * width, (c + 1) * width)
                 entries = tree_offsets[i][:, c * width // LIST_GROUP : (c + 1) * width // LIST_GROUP]
                 if i == 0:
@@ -179,54 +247,71 @@ def tile_picked_ymedu_logs_p_kernel(
                     nc.sync.dma_start(out=out[m * P : (m + 1) * P, cols], in_=acc[:])
             total[m] = acc
 
+        on_vector = nc.vector.tensor_copy
+        on_scalar = nc.scalar.copy
         gather_words(0)
         nc.vector.tensor_copy(picked_scales[:], scale_rows[:].indirect(offsets[:]))
-        interleave(0, 0, nc.vector.tensor_copy)
-        quantize(0, 0)
         gather_words(1)
+        interleave(0, 0, on_vector, 0, P)
+        interleave(0, 0, on_scalar, P, V)
+        quantize(0, 0)
         for m in range(ROW_TILES):
-            multiply(0, m, 0)
-        interleave(0, 1, nc.vector.tensor_copy, 0, P)
-        interleave(0, 1, nc.scalar.copy, P, V)
+            interleave(0, 1, on_vector, m * P, m * P + P // 2)
+            interleave(0, 1, on_scalar, m * P + P // 2, (m + 1) * P)
         for m in range(ROW_TILES):
             quantize(0, 1, m * P, (m + 1) * P)
-            multiply(0, m, 1)
-
-        interleave(1, 0, nc.scalar.copy)
-        row_max(0, 0)
-        row_max(0, 1)
-        sum_of_exps(0, 0)
+            for g in range(PASSES):
+                multiply(0, m, g)
+        interleave(1, 0, on_vector, 0, 192)
+        interleave(1, 0, on_scalar, 192, V)
+        row_max_and_copy(0, 0)
         quantize(1, 0)
-        interleave(1, 1, nc.scalar.copy, 0, P)
-        interleave(1, 1, nc.vector.tensor_copy, P, V)
+        interleave(1, 1, on_scalar)
+        row_max_and_copy(0, 1)
+        sum_of_exps(0, 0)
         quantize(1, 1)
         for g in range(PASSES):
             for m in range(ROW_TILES):
                 multiply(1, m, g)
-
-        for g in range(PASSES):
-            for m in range(ROW_TILES):
-                interleave(2, g, nc.vector.tensor_copy, m * P, (m + 1) * P)
-            for m in range(ROW_TILES):
-                quantize(2, g, m * P, (m + 1) * P)
-            row_max(1, g)
-        for g in range(PASSES):
+        quadrature(0, 0)
+        row_bias_on(nc.gpsimd, 0, 0)
+        interleave(2, 0, on_scalar)
+        interleave(2, 1, on_vector)
+        sum_of_exps(0, 1)
+        row_max_and_copy(1, 0)
+        logp_from_copy(nc.gpsimd, 0, 0)
+        quantize(2, 1)
+        quantize(2, 0)
+        for g in reversed(range(PASSES)):
             for m in range(ROW_TILES):
                 multiply(2, m, g)
+        row_max_and_copy(1, 1)
+        sum_of_exps(1, 0)
+        quadrature(0, 1)
+        row_bias_on(nc.gpsimd, 0, 1)
+        logp_from_copy(nc.gpsimd, 0, 1)
+        quadrature(1, 0)
+        row_bias_on(nc.gpsimd, 1, 0)
+        logp_from_copy(nc.gpsimd, 1, 0)
+        fetch(0, 0)
         row_max(2, 0)
         row_max(2, 1)
-
-        for i in range(HEADS):
-            quadrature(i, 0)
-            sum_of_exps(i, 1)
-            row_bias(i, 0)
-            quadrature(i, 1)
-            log_probabilities(i, 0)
-            row_bias(i, 1)
-            if i < LAST_HEAD:
-                sum_of_exps(i + 1, 0)
-            log_probabilities(i, 1)
-
-        for i in range(HEADS):
-            for m in range(ROW_TILES):
-                fetch(i, m, 2 if (i, m) == (LAST_HEAD, ROW_TILES - 1) else 1)
+        sum_of_exps(1, 1)
+        sum_of_exps(2, 0)
+        quadrature(1, 1)
+        row_bias_on(nc.gpsimd, 1, 1)
+        logp_from_copy(nc.gpsimd, 1, 1)
+        sum_of_exps(2, 1)
+        quadrature(2, 0)
+        shift(2, 0)
+        shift(2, 1)
+        quadrature(2, 1)
+        row_bias(2, 0)
+        row_bias(2, 1)
+        logp_on_scalar(2, 0)
+        logp_on_scalar(2, 1)
+        fetch(0, 1)
+        fetch(1, 0)
+        fetch(1, 1)
+        fetch(2, 0)
+        fetch(2, 1, 2)

@@ -28,9 +28,9 @@ LIST_GROUP = 16
 RUN = 4
 LAST_HEAD = HEADS - 1
 
-NODES = 64
-STEP = 0.46
-FIRST = -26.4
+NODES = 68
+STEP = 0.42
+FIRST = -25.8
 
 NEG_MAX, SUM, SHIFT, QUAD, BIAS = range(5)
 
@@ -41,7 +41,14 @@ def tile_picked_ymedu_logs_p_kernel(
     nc = tc.nc
     heads = (h0, h1, h2)
     trees = (tree1, tree2, tree3)
-    rule_at_one = STEP * sum(math.e ** -(math.e ** (FIRST + STEP * n)) for n in range(NODES))
+    low, high = 0.0, 1.0
+    for halving in range(60):
+        offset = (low + high) / 2
+        if sum(math.tanh(math.e ** (FIRST + STEP * n) - offset) for n in range(NODES)) > 0:
+            low = offset
+        else:
+            high = offset
+    weight = STEP / (1 + math.tanh(offset))
 
     with ExitStack() as ctx:
         keep = ctx.enter_context(tc.tile_pool(name="keep", bufs=1))
@@ -81,30 +88,37 @@ def tile_picked_ymedu_logs_p_kernel(
         def load_words(g):
             nc.sync.dma_start(out=words[g][:], in_=x_words[g].rearrange("p n b -> p (n b)").bitcast(I32))
 
-        scale_rows = keep.tile([P, T], U8, name="scale_rows", align_bytes=64)
-        picked_scales = keep.tile([P, S], U8, name="picked_scales", align_bytes=64)
-        nc.vector.memset(scale_rows[:].bitcast(I32), 0)
+        scale_rows = keep.tile([P, PASSES * T], U8, name="scale_rows", align_bytes=64)
+        picked_scales = keep.tile([P, PASSES * S], U8, name="picked_scales", align_bytes=64)
+        x_planes = keep.tile([P, PASSES * S], U8, name="x_planes", align_bytes=64)
+        nc.vector.memset(scale_rows[:, :T].bitcast(I32), 0)
+        nc.gpsimd.memset(scale_rows[:, T:].bitcast(I32), 0)
         nc.sync.dma_start(offsets[:], offs)
-        load_words(0)
-        for q in range(QUADRANTS):
-            nc.sync.dma_start(
-                out=scale_rows[32 * q : 32 * q + SCALE_ROWS * PASSES, :].bitcast(I32),
-                in_=x_scales[:, SCALE_ROWS * q : SCALE_ROWS * (q + 1), :].bitcast(I32),
+        load_head(0, 0)
+        nc.sync.dma_start(
+            out=scale_rows[0:P:8, :].bitcast(I32).rearrange("r (g n) -> r g n", g=PASSES),
+            in_=x_scales.bitcast(I32).rearrange("g r n -> r g n"),
+        )
+        for g in range(PASSES):
+            load_words(g)
+        load_head(0, 1)
+        for g in range(PASSES):
+            nc.vector.tensor_copy(
+                picked_scales[:, g * S : (g + 1) * S], scale_rows[:, g * T : (g + 1) * T].indirect(offsets[:])
             )
-        load_words(1)
-        for i in range(HEADS):
+        nc.vector.tensor_copy(x_planes[:].bitcast(I32), picked_scales[:].bitcast(I32))
+        for r in range(1, SCALE_ROWS):
+            nc.sync.dma_start(out=x_planes[r:P:32, :].bitcast(I32), in_=picked_scales[8 * r : P : 32, :].bitcast(I32))
+        for i in range(1, HEADS):
             for g in range(PASSES):
                 load_head(i, g)
         for i in range(HEADS):
             nc.sync.dma_start(tree_offsets[i][:], trees[i])
 
-
         count = keep.tile([P, NODES], F32, name="count")
         nc.gpsimd.iota(count[:], [[1, NODES]], base=0, channel_multiplier=0, allow_small_or_imprecise_dtypes=True)
         nodes = keep.tile([P, NODES], F32, name="nodes")
         nc.scalar.activation(nodes[:], count[:], ACT.Exp, scale=STEP, bias=FIRST)
-        neg_nodes = keep.tile([P, NODES], F32, name="neg_nodes")
-        nc.scalar.activation(neg_nodes[:], nodes[:], ACT.Copy, scale=-1.0)
 
         picked_words = [keep.tile([P, S], U32, name="picked_words%d" % g, align_bytes=64) for g in range(PASSES)]
         codes = [
@@ -148,18 +162,18 @@ def tile_picked_ymedu_logs_p_kernel(
                 lhsT=codes[i][g][:, cols].bitcast(FP8X4),
                 lhsT_scale=planes[i][g][:, cols],
                 rhs=picked_words[g][:].bitcast(FP8X4),
-                rhs_scale=picked_scales[SCALE_ROWS * g : P, :],
+                rhs_scale=x_planes[:, g * S : (g + 1) * S],
                 start=first,
                 stop=not first,
             )
 
         held = {
             "stats0_0": ("raw", 1, 0, 0),
-            "exps0_0": ("raw", 1, 1, 0),
+            "stats0_1": ("raw", 1, 1, 0),
             "terms0_0": ("grouped", 2, 0, 0),
             "exps0_1": ("raw", 2, 0, 0),
+            "logp0_0": ("raw", 2, 0, 2048),
             "stats1_0": ("raw", 2, 1, 2048),
-            "logp0_0": ("raw", 2, 1, 0),
             "stats1_1": ("grouped", 2, 1, 0),
             "total0_0_0": ("grouped", 2, 1, 512),
         }
@@ -193,28 +207,20 @@ def tile_picked_ymedu_logs_p_kernel(
                 exps[:], banks[i, m][:], ACT.Exp, bias=column(i, m, NEG_MAX), accum_out=column(i, m, SUM)
             )
 
-        def shift(i, m):
-            nc.scalar.activation(column(i, m, SHIFT), column(i, m, NEG_MAX), ACT.Identity, bias=-rule_at_one)
-
         def quadrature(i, m):
             label = "terms%d_%d" % (i, m)
             terms = new_tile([P, NODES], label)
             nc.scalar.activation(
                 terms[:],
-                neg_nodes[:],
-                ACT.Exp,
+                nodes[:],
+                ACT.Tanh,
                 scale=column(i, m, SUM),
-                bias=math.log10(STEP) / math.log10(math.e),
+                bias=-offset,
                 accum_out=column(i, m, QUAD),
             )
 
         def row_bias(i, m):
-            nc.scalar.activation(column(i, m, BIAS), column(i, m, QUAD), ACT.Identity, bias=column(i, m, SHIFT))
-
-        def row_bias_on(engine, i, m):
-            engine.tensor_scalar(
-                column(i, m, BIAS), column(i, m, QUAD), column(i, m, NEG_MAX), -rule_at_one, ALU.add, ALU.add
-            )
+            nc.scalar.activation(column(i, m, BIAS), column(i, m, QUAD), ACT.Identity, scale=-weight, bias=column(i, m, NEG_MAX))
 
         def new_logp(i, m):
             label = "logp%d_%d" % (i, m)
@@ -226,11 +232,6 @@ def tile_picked_ymedu_logs_p_kernel(
 
         def logp_from_copy(engine, i, m):
             engine.tensor_scalar(new_logp(i, m), negated[i, m][:], -1.0, column(i, m, BIAS), ALU.mult, ALU.add)
-
-        def logp_from_bank(i, m):
-            nc.vector.tensor_scalar(
-                new_logp(i, m), banks[i, m][:], column(i, m, SHIFT), column(i, m, QUAD), ALU.add, ALU.add
-            )
 
         def fetch(i, m, pieces=1):
             width = U // pieces
@@ -249,12 +250,10 @@ def tile_picked_ymedu_logs_p_kernel(
 
         on_vector = nc.vector.tensor_copy
         on_scalar = nc.scalar.copy
-        gather_words(0)
-        nc.vector.tensor_copy(picked_scales[:], scale_rows[:].indirect(offsets[:]))
-        gather_words(1)
-        interleave(0, 0, on_vector, 0, P)
-        interleave(0, 0, on_scalar, P, V)
+        interleave(0, 0, on_scalar)
         quantize(0, 0)
+        gather_words(0)
+        gather_words(1)
         for m in range(ROW_TILES):
             interleave(0, 1, on_vector, m * P, m * P + P // 2)
             interleave(0, 1, on_scalar, m * P + P // 2, (m + 1) * P)
@@ -264,54 +263,52 @@ def tile_picked_ymedu_logs_p_kernel(
                 multiply(0, m, g)
         interleave(1, 0, on_vector, 0, 192)
         interleave(1, 0, on_scalar, 192, V)
-        row_max_and_copy(0, 0)
+        row_max(0, 0)
+        interleave(1, 1, on_vector)
         quantize(1, 0)
-        interleave(1, 1, on_scalar)
-        row_max_and_copy(0, 1)
+        row_max(0, 1)
         sum_of_exps(0, 0)
         quantize(1, 1)
         for g in range(PASSES):
             for m in range(ROW_TILES):
                 multiply(1, m, g)
         quadrature(0, 0)
-        row_bias_on(nc.gpsimd, 0, 0)
         interleave(2, 0, on_scalar)
         interleave(2, 1, on_vector)
+        row_bias(0, 0)
         sum_of_exps(0, 1)
-        row_max_and_copy(1, 0)
-        logp_from_copy(nc.gpsimd, 0, 0)
+        row_max(1, 0)
         quantize(2, 1)
         quantize(2, 0)
         for g in reversed(range(PASSES)):
             for m in range(ROW_TILES):
                 multiply(2, m, g)
         row_max_and_copy(1, 1)
-        sum_of_exps(1, 0)
+        logp_on_scalar(0, 0)
         quadrature(0, 1)
-        row_bias_on(nc.gpsimd, 0, 1)
-        logp_from_copy(nc.gpsimd, 0, 1)
+        sum_of_exps(1, 0)
+        row_bias(0, 1)
         quadrature(1, 0)
-        row_bias_on(nc.gpsimd, 1, 0)
-        logp_from_copy(nc.gpsimd, 1, 0)
+        logp_on_scalar(0, 1)
+        row_bias(1, 0)
         fetch(0, 0)
         row_max(2, 0)
         row_max(2, 1)
         sum_of_exps(1, 1)
-        sum_of_exps(2, 0)
+        logp_on_scalar(1, 0)
         quadrature(1, 1)
-        row_bias_on(nc.gpsimd, 1, 1)
-        logp_from_copy(nc.gpsimd, 1, 1)
-        sum_of_exps(2, 1)
+        sum_of_exps(2, 0)
+        row_bias(1, 1)
         quadrature(2, 0)
-        shift(2, 0)
-        shift(2, 1)
-        quadrature(2, 1)
+        sum_of_exps(2, 1)
         row_bias(2, 0)
-        row_bias(2, 1)
+        quadrature(2, 1)
         logp_on_scalar(2, 0)
+        row_bias(2, 1)
         logp_on_scalar(2, 1)
         fetch(0, 1)
         fetch(1, 0)
+        logp_from_copy(nc.vector, 1, 1)
         fetch(1, 1)
         fetch(2, 0)
         fetch(2, 1, 2)

@@ -25,7 +25,7 @@ ROW_TILES = V // P
 QUADRANTS = 4
 SCALE_ROWS = 4
 LIST_GROUP = 16
-RUN = 4
+RUN = 2
 LAST_HEAD = HEADS - 1
 
 NODES = 68
@@ -93,8 +93,8 @@ def tile_picked_ymedu_logs_p_kernel(
         x_planes = keep.tile([P, PASSES * S], U8, name="x_planes", align_bytes=64)
         nc.vector.memset(scale_rows[:, :T].bitcast(I32), 0)
         nc.gpsimd.memset(scale_rows[:, T:].bitcast(I32), 0)
-        nc.sync.dma_start(offsets[:], offs)
         load_head(0, 0)
+        nc.sync.dma_start(offsets[:], offs)
         nc.sync.dma_start(
             out=scale_rows[0:P:8, :].bitcast(I32).rearrange("r (g n) -> r g n", g=PASSES),
             in_=x_scales.bitcast(I32).rearrange("g r n -> r g n"),

@@ -22,17 +22,35 @@ PACK = 4
 K_PASS = P * PACK
 PASSES = K // K_PASS
 ROW_TILES = V // P
-QUADRANTS = 4
+QUADRANT = 32
 SCALE_ROWS = 4
+ROW_STEP = QUADRANT // SCALE_ROWS
 LIST_GROUP = 16
 RUN = 2
 LAST_HEAD = HEADS - 1
 
+VECTOR_COLUMNS = 192
+
 NODES = 68
 STEP = 0.42
 FIRST = -25.8
+HALVINGS = 60
 
-NEG_MAX, SUM, SHIFT, QUAD, BIAS = range(5)
+NEG_MAX, SUM, QUAD, BIAS = range(4)
+
+RAW_BYTES = PACK * V * 4
+GROUPED_BYTES = PACK * V * 2
+
+
+def vanishing_offset():
+    low, high = 0.0, 1.0
+    for halving in range(HALVINGS):
+        middle = (low + high) / 2
+        if sum(math.tanh(math.e ** (FIRST + STEP * n) - middle) for n in range(NODES)) > 0:
+            low = middle
+        else:
+            high = middle
+    return (low + high) / 2
 
 
 def tile_picked_ymedu_logs_p_kernel(
@@ -41,74 +59,86 @@ def tile_picked_ymedu_logs_p_kernel(
     nc = tc.nc
     heads = (h0, h1, h2)
     trees = (tree1, tree2, tree3)
-    low, high = 0.0, 1.0
-    for halving in range(60):
-        offset = (low + high) / 2
-        if sum(math.tanh(math.e ** (FIRST + STEP * n) - offset) for n in range(NODES)) > 0:
-            low = offset
-        else:
-            high = offset
-    weight = STEP / (1 + math.tanh(offset))
+    tanh_offset = vanishing_offset()
+    log_factor = STEP / (1 + math.tanh(tanh_offset))
 
     with ExitStack() as ctx:
         keep = ctx.enter_context(tc.tile_pool(name="keep", bufs=1))
         staged = ctx.enter_context(tc.tile_pool(name="staged", bufs=1))
         psum = ctx.enter_context(tc.psum_pool(name="psum", bufs=1))
 
-        def per_head_and_pass(label, shape, dtype):
-            return [
-                [keep.tile(shape, dtype, name="%s%d_%d" % (label, i, g), align_bytes=64) for g in range(PASSES)]
-                for i in range(HEADS)
-            ]
+        def raw_at(i, g):
+            return (PASSES * i + g) * (RAW_BYTES + GROUPED_BYTES)
+
+        def grouped_at(i, g):
+            return raw_at(i, g) + RAW_BYTES
+
+        shared = {
+            "stats0_0": raw_at(1, 0),
+            "stats0_1": raw_at(1, 1),
+            "stats1_0": raw_at(2, 1),
+            "codes2_0": raw_at(2, 1) + RAW_BYTES // 2,
+            "terms0_0": grouped_at(2, 0),
+            "exps0_1": raw_at(2, 0),
+            "logp0_0": grouped_at(1, 1),
+            "logp1_0": grouped_at(1, 1),
+            "stats1_1": grouped_at(2, 1),
+            "total0_0_0": grouped_at(2, 1) + GROUPED_BYTES // 2,
+        }
+
+        def new_tile(shape, dtype, label):
+            if label in shared:
+                return staged.tile(shape, dtype, name=label, offset=shared[label], align_bytes=64)
+            return keep.tile(shape, dtype, name=label, align_bytes=64)
+
+        pairs = [(i, g) for i in range(HEADS) for g in range(PASSES)]
+        raw = {
+            (i, g): staged.tile([P, PACK, V], F32, name="raw%d_%d" % (i, g), offset=raw_at(i, g), align_bytes=64)
+            for i, g in pairs
+        }
+        grouped = {
+            (i, g): staged.tile(
+                [P, V * PACK], BF16, name="grouped%d_%d" % (i, g), offset=grouped_at(i, g), align_bytes=64
+            )
+            for i, g in pairs
+        }
+        codes = {(i, g): new_tile([P, V], U32, "codes%d_%d" % (i, g)) for i, g in pairs}
+        planes = {(i, g): new_tile([P, V], U8, "planes%d_%d" % (i, g)) for i, g in pairs}
 
         offsets = keep.tile([P, S // LIST_GROUP], U16, name="offsets")
         tree_offsets = [keep.tile([P, U // LIST_GROUP], U16, name="tree%d" % i) for i in range(HEADS)]
-        words = [keep.tile([P, T], I32, name="words%d" % g, align_bytes=64) for g in range(PASSES)]
-
-        def staged_tiles(label, shape, dtype):
-            return [
-                [
-                    staged.tile(shape, dtype, name="%s%d_%d" % (label, i, g), offset=place[label, i, g], align_bytes=64)
-                    for g in range(PASSES)
-                ]
-                for i in range(HEADS)
-            ]
-
-        place = {}
-        for i in range(HEADS):
-            for g in range(PASSES):
-                place["raw", i, g] = (PASSES * i + g) * 6144
-                place["grouped", i, g] = place["raw", i, g] + 4096
-        raw = staged_tiles("raw", [P, PACK, V], F32)
+        words = [new_tile([P, T], I32, "words%d" % g) for g in range(PASSES)]
+        picked_words = [new_tile([P, S], U32, "picked_words%d" % g) for g in range(PASSES)]
+        scale_rows = new_tile([P, PASSES * T], U8, "scale_rows")
+        picked_rows = new_tile([P, PASSES * S], U8, "picked_rows")
+        picked_planes = new_tile([P, PASSES * S], U8, "picked_planes")
 
         def load_head(i, g):
             rows = heads[i][g * K_PASS : (g + 1) * K_PASS, :]
-            nc.sync.dma_start(out=raw[i][g][:], in_=rows.rearrange("(p j) t -> p j t", j=PACK))
+            nc.sync.dma_start(out=raw[i, g][:], in_=rows.rearrange("(p j) t -> p j t", j=PACK))
 
-        def load_words(g):
-            nc.sync.dma_start(out=words[g][:], in_=x_words[g].rearrange("p n b -> p (n b)").bitcast(I32))
-
-        scale_rows = keep.tile([P, PASSES * T], U8, name="scale_rows", align_bytes=64)
-        picked_scales = keep.tile([P, PASSES * S], U8, name="picked_scales", align_bytes=64)
-        x_planes = keep.tile([P, PASSES * S], U8, name="x_planes", align_bytes=64)
         nc.vector.memset(scale_rows[:, :T].bitcast(I32), 0)
         nc.gpsimd.memset(scale_rows[:, T:].bitcast(I32), 0)
         load_head(0, 0)
         nc.sync.dma_start(offsets[:], offs)
         nc.sync.dma_start(
-            out=scale_rows[0:P:8, :].bitcast(I32).rearrange("r (g n) -> r g n", g=PASSES),
+            out=scale_rows[0:P:ROW_STEP, :].bitcast(I32).rearrange("r (g n) -> r g n", g=PASSES),
             in_=x_scales.bitcast(I32).rearrange("g r n -> r g n"),
         )
         for g in range(PASSES):
-            load_words(g)
+            nc.sync.dma_start(out=words[g][:], in_=x_words[g].rearrange("p n b -> p (n b)").bitcast(I32))
         load_head(0, 1)
+
         for g in range(PASSES):
-            nc.vector.tensor_copy(
-                picked_scales[:, g * S : (g + 1) * S], scale_rows[:, g * T : (g + 1) * T].indirect(offsets[:])
+            window = scale_rows[:, g * T : (g + 1) * T]
+            nc.vector.tensor_copy(picked_rows[:, g * S : (g + 1) * S], window.indirect(offsets[:]))
+        nc.vector.tensor_copy(picked_planes[:].bitcast(I32), picked_rows[:].bitcast(I32))
+        for s in range(1, SCALE_ROWS):
+            nc.sync.dma_start(
+                out=picked_planes[s:P:QUADRANT, :].bitcast(I32),
+                in_=picked_rows[ROW_STEP * s : P : QUADRANT, :].bitcast(I32),
             )
-        nc.vector.tensor_copy(x_planes[:].bitcast(I32), picked_scales[:].bitcast(I32))
-        for r in range(1, SCALE_ROWS):
-            nc.sync.dma_start(out=x_planes[r:P:32, :].bitcast(I32), in_=picked_scales[8 * r : P : 32, :].bitcast(I32))
+
         for i in range(1, HEADS):
             for g in range(PASSES):
                 load_head(i, g)
@@ -120,30 +150,20 @@ def tile_picked_ymedu_logs_p_kernel(
         nodes = keep.tile([P, NODES], F32, name="nodes")
         nc.scalar.activation(nodes[:], count[:], ACT.Exp, scale=STEP, bias=FIRST)
 
-        picked_words = [keep.tile([P, S], U32, name="picked_words%d" % g, align_bytes=64) for g in range(PASSES)]
-        codes = [
-            [keep.tile([P, V], U32, name="codes%d_%d" % (i, g), align_bytes=64) if (i, g) != (2, 0) else None for g in range(PASSES)]
-            for i in range(HEADS)
-        ]
-        planes = per_head_and_pass("planes", [P, V], U8)
-        grouped = staged_tiles("grouped", [P, V * PACK], BF16)
-
-        codes[2][0] = staged.tile([P, V], U32, name="held_codes", offset=place["raw", 2, 1] + 2048 + 1024, align_bytes=64)
-
-        def gather_words(g):
-            nc.vector.tensor_copy(picked_words[g][:], words[g][:].bitcast(U32).indirect(offsets[:]))
+        on_vector = nc.vector.tensor_copy
+        on_scalar = nc.scalar.copy
 
         def interleave(i, g, copy, lo=0, hi=V):
             copy(
-                grouped[i][g][:, PACK * lo : PACK * hi].rearrange("p (c n j) -> p c j n", n=RUN, j=PACK),
-                raw[i][g][:, :, lo:hi].rearrange("p j (c n) -> p c j n", n=RUN),
+                grouped[i, g][:, PACK * lo : PACK * hi].rearrange("p (c n j) -> p c j n", n=RUN, j=PACK),
+                raw[i, g][:, :, lo:hi].rearrange("p j (c n) -> p c j n", n=RUN),
             )
 
         def quantize(i, g, lo=0, hi=V):
             nc.vector.quantize_mx(
-                out=codes[i][g][:, lo:hi].bitcast(FP8X4),
-                scales=planes[i][g][:, lo:hi],
-                in_=grouped[i][g][:, PACK * lo : PACK * hi],
+                out=codes[i, g][:, lo:hi].bitcast(FP8X4),
+                scales=planes[i, g][:, lo:hi],
+                in_=grouped[i, g][:, PACK * lo : PACK * hi],
             )
 
         banks = {}
@@ -159,85 +179,66 @@ def tile_picked_ymedu_logs_p_kernel(
             cols = slice(m * P, (m + 1) * P)
             nc.tensor.matmul_mx(
                 out=banks[i, m][:],
-                lhsT=codes[i][g][:, cols].bitcast(FP8X4),
-                lhsT_scale=planes[i][g][:, cols],
+                lhsT=codes[i, g][:, cols].bitcast(FP8X4),
+                lhsT_scale=planes[i, g][:, cols],
                 rhs=picked_words[g][:].bitcast(FP8X4),
-                rhs_scale=x_planes[:, g * S : (g + 1) * S],
+                rhs_scale=picked_planes[:, g * S : (g + 1) * S],
                 start=first,
                 stop=not first,
             )
 
-        held = {
-            "stats0_0": ("raw", 1, 0, 0),
-            "stats0_1": ("raw", 1, 1, 0),
-            "terms0_0": ("grouped", 2, 0, 0),
-            "exps0_1": ("raw", 2, 0, 0),
-            "logp0_0": ("raw", 2, 0, 2048),
-            "stats1_0": ("raw", 2, 1, 2048),
-            "stats1_1": ("grouped", 2, 1, 0),
-            "total0_0_0": ("grouped", 2, 1, 512),
-        }
-
-        def new_tile(shape, label):
-            if label in held:
-                kind, i, g, within = held[label]
-                return staged.tile(shape, F32, name=label, offset=place[kind, i, g] + within, align_bytes=64)
-            return keep.tile(shape, F32, name=label, align_bytes=64)
-
         def column(i, m, c):
-            return stats[i, m][:, 8 * c : 8 * c + 1]
+            return stats[i, m][:, c : c + 1]
 
         def row_max(i, m):
-            label = "stats%d_%d" % (i, m)
-            stats[i, m] = new_tile([P, 40], label)
+            stats[i, m] = new_tile([P, 4], F32, "stats%d_%d" % (i, m))
             nc.vector.tensor_reduce(column(i, m, NEG_MAX), banks[i, m][:], mybir.AxisListType.X, ALU.max, negate=True)
 
         def row_max_and_copy(i, m):
-            label = "stats%d_%d" % (i, m)
-            stats[i, m] = new_tile([P, 40], label)
-            negated[i, m] = keep.tile([P, S], F32, name="negated%d_%d" % (i, m))
+            stats[i, m] = new_tile([P, 4], F32, "stats%d_%d" % (i, m))
+            negated[i, m] = new_tile([P, S], F32, "negated%d_%d" % (i, m))
             nc.vector.tensor_scalar(
                 negated[i, m][:], banks[i, m][:], -1.0, None, ALU.mult, ALU.min, accum_out=column(i, m, NEG_MAX)
             )
 
         def sum_of_exps(i, m):
-            label = "exps%d_%d" % (i, m)
-            exps = new_tile([P, S], label)
+            exps = new_tile([P, S], F32, "exps%d_%d" % (i, m))
             nc.scalar.activation(
                 exps[:], banks[i, m][:], ACT.Exp, bias=column(i, m, NEG_MAX), accum_out=column(i, m, SUM)
             )
 
         def quadrature(i, m):
-            label = "terms%d_%d" % (i, m)
-            terms = new_tile([P, NODES], label)
+            terms = new_tile([P, NODES], F32, "terms%d_%d" % (i, m))
             nc.scalar.activation(
                 terms[:],
                 nodes[:],
                 ACT.Tanh,
                 scale=column(i, m, SUM),
-                bias=-offset,
+                bias=-tanh_offset,
                 accum_out=column(i, m, QUAD),
             )
 
         def row_bias(i, m):
-            nc.scalar.activation(column(i, m, BIAS), column(i, m, QUAD), ACT.Identity, scale=-weight, bias=column(i, m, NEG_MAX))
-
-        def new_logp(i, m):
-            label = "logp%d_%d" % (i, m)
-            logp[i, m] = new_tile([P, S], label)
-            return logp[i, m][:]
+            nc.scalar.activation(
+                column(i, m, BIAS), column(i, m, QUAD), ACT.Identity, scale=-log_factor, bias=column(i, m, NEG_MAX)
+            )
 
         def logp_on_scalar(i, m):
-            nc.scalar.activation(new_logp(i, m), banks[i, m][:], ACT.Identity, bias=column(i, m, BIAS))
+            logp[i, m] = new_tile([P, S], F32, "logp%d_%d" % (i, m))
+            nc.scalar.activation(logp[i, m][:], banks[i, m][:], ACT.Identity, bias=column(i, m, BIAS))
 
-        def logp_from_copy(engine, i, m):
-            engine.tensor_scalar(new_logp(i, m), negated[i, m][:], -1.0, column(i, m, BIAS), ALU.mult, ALU.add)
+        def logp_on_gpsimd(i, m):
+            logp[i, m] = new_tile([P, S], F32, "logp%d_%d" % (i, m))
+            nc.gpsimd.tensor_scalar(logp[i, m][:], negated[i, m][:], -1.0, column(i, m, BIAS), ALU.mult, ALU.add)
+
+        def logp_on_vector(i, m):
+            logp[i, m] = new_tile([P, S], F32, "logp%d_%d" % (i, m))
+            nc.vector.tensor_scalar(logp[i, m][:], negated[i, m][:], -1.0, column(i, m, BIAS), ALU.mult, ALU.add)
 
         def fetch(i, m, pieces=1):
             width = U // pieces
             for c in range(pieces):
-                label = "total%d_%d_%d" % (i, m, c)
-                acc = new_tile([P, width], label)
+                acc = new_tile([P, width], F32, "total%d_%d_%d" % (i, m, c))
                 cols = slice(c * width, (c + 1) * width)
                 entries = tree_offsets[i][:, c * width // LIST_GROUP : (c + 1) * width // LIST_GROUP]
                 if i == 0:
@@ -248,12 +249,10 @@ def tile_picked_ymedu_logs_p_kernel(
                     nc.sync.dma_start(out=out[m * P : (m + 1) * P, cols], in_=acc[:])
             total[m] = acc
 
-        on_vector = nc.vector.tensor_copy
-        on_scalar = nc.scalar.copy
         interleave(0, 0, on_scalar)
         quantize(0, 0)
-        gather_words(0)
-        gather_words(1)
+        for g in range(PASSES):
+            nc.vector.tensor_copy(picked_words[g][:], words[g][:].bitcast(U32).indirect(offsets[:]))
         for m in range(ROW_TILES):
             interleave(0, 1, on_vector, m * P, m * P + P // 2)
             interleave(0, 1, on_scalar, m * P + P // 2, (m + 1) * P)
@@ -261,30 +260,33 @@ def tile_picked_ymedu_logs_p_kernel(
             quantize(0, 1, m * P, (m + 1) * P)
             for g in range(PASSES):
                 multiply(0, m, g)
-        interleave(1, 0, on_vector, 0, 192)
-        interleave(1, 0, on_scalar, 192, V)
-        row_max(0, 0)
+
+        interleave(1, 0, on_vector, 0, VECTOR_COLUMNS)
+        interleave(1, 0, on_scalar, VECTOR_COLUMNS, V)
+        row_max_and_copy(0, 0)
         interleave(1, 1, on_vector)
         quantize(1, 0)
+        quantize(1, 1)
         row_max(0, 1)
         sum_of_exps(0, 0)
-        quantize(1, 1)
         for g in range(PASSES):
             for m in range(ROW_TILES):
                 multiply(1, m, g)
+
         quadrature(0, 0)
+        row_bias(0, 0)
+        logp_on_gpsimd(0, 0)
         interleave(2, 0, on_scalar)
         interleave(2, 1, on_vector)
-        row_bias(0, 0)
         sum_of_exps(0, 1)
-        row_max(1, 0)
-        quantize(2, 1)
-        quantize(2, 0)
+        row_max_and_copy(1, 0)
+        for g in reversed(range(PASSES)):
+            quantize(2, g)
         for g in reversed(range(PASSES)):
             for m in range(ROW_TILES):
                 multiply(2, m, g)
+
         row_max_and_copy(1, 1)
-        logp_on_scalar(0, 0)
         quadrature(0, 1)
         sum_of_exps(1, 0)
         row_bias(0, 1)
@@ -294,8 +296,8 @@ def tile_picked_ymedu_logs_p_kernel(
         fetch(0, 0)
         row_max(2, 0)
         row_max(2, 1)
+        logp_on_gpsimd(1, 0)
         sum_of_exps(1, 1)
-        logp_on_scalar(1, 0)
         quadrature(1, 1)
         sum_of_exps(2, 0)
         row_bias(1, 1)
@@ -306,9 +308,10 @@ def tile_picked_ymedu_logs_p_kernel(
         logp_on_scalar(2, 0)
         row_bias(2, 1)
         logp_on_scalar(2, 1)
+
         fetch(0, 1)
+        logp_on_vector(1, 1)
         fetch(1, 0)
-        logp_from_copy(nc.vector, 1, 1)
         fetch(1, 1)
         fetch(2, 0)
-        fetch(2, 1, 2)
+        fetch(2, 1, pieces=2)

@@ -40,6 +40,7 @@ NEG_MAX, SUM, QUAD, BIAS = range(4)
 
 RAW_BYTES = PACK * V * 4
 GROUPED_BYTES = PACK * V * 2
+TERMS_OVERLAP = 128
 
 
 def vanishing_offset():
@@ -73,17 +74,21 @@ def tile_picked_ymedu_logs_p_kernel(
         def grouped_at(i, g):
             return raw_at(i, g) + RAW_BYTES
 
+        half_raw = RAW_BYTES // 2
         shared = {
             "stats0_0": raw_at(1, 0),
             "stats0_1": raw_at(1, 1),
-            "stats1_0": raw_at(2, 1),
-            "codes2_0": raw_at(2, 1) + RAW_BYTES // 2,
-            "terms0_0": grouped_at(2, 0),
-            "exps0_1": raw_at(2, 0),
-            "logp0_0": grouped_at(1, 1),
-            "logp1_0": grouped_at(1, 1),
+            "stats1_0": raw_at(2, 0) + half_raw,
+            "exps0_1": raw_at(2, 1),
             "stats1_1": grouped_at(2, 1),
             "total0_0_0": grouped_at(2, 1) + GROUPED_BYTES // 2,
+            "terms0_0": grouped_at(2, 0),
+            "codes2_0": raw_at(2, 1) + half_raw,
+            "logp0_0": grouped_at(1, 1),
+            "logp1_0": grouped_at(1, 1),
+            "terms1_0": raw_at(0, 0) + half_raw - TERMS_OVERLAP,
+            "exps1_1": raw_at(0, 0),
+            "logp0_1": raw_at(0, 0) + half_raw,
         }
 
         def new_tile(shape, dtype, label):
@@ -227,13 +232,9 @@ def tile_picked_ymedu_logs_p_kernel(
             logp[i, m] = new_tile([P, S], F32, "logp%d_%d" % (i, m))
             nc.scalar.activation(logp[i, m][:], banks[i, m][:], ACT.Identity, bias=column(i, m, BIAS))
 
-        def logp_on_gpsimd(i, m):
+        def logp_from_copy(i, m, engine):
             logp[i, m] = new_tile([P, S], F32, "logp%d_%d" % (i, m))
-            nc.gpsimd.tensor_scalar(logp[i, m][:], negated[i, m][:], -1.0, column(i, m, BIAS), ALU.mult, ALU.add)
-
-        def logp_on_vector(i, m):
-            logp[i, m] = new_tile([P, S], F32, "logp%d_%d" % (i, m))
-            nc.vector.tensor_scalar(logp[i, m][:], negated[i, m][:], -1.0, column(i, m, BIAS), ALU.mult, ALU.add)
+            engine.tensor_scalar(logp[i, m][:], negated[i, m][:], -1.0, column(i, m, BIAS), ALU.mult, ALU.add)
 
         def fetch(i, m, pieces=1):
             width = U // pieces
@@ -275,9 +276,10 @@ def tile_picked_ymedu_logs_p_kernel(
 
         quadrature(0, 0)
         row_bias(0, 0)
-        logp_on_gpsimd(0, 0)
+        logp_from_copy(0, 0, nc.gpsimd)
         interleave(2, 0, on_scalar)
-        interleave(2, 1, on_vector)
+        interleave(2, 1, on_vector, 0, VECTOR_COLUMNS)
+        interleave(2, 1, on_scalar, VECTOR_COLUMNS, V)
         sum_of_exps(0, 1)
         row_max_and_copy(1, 0)
         for g in reversed(range(PASSES)):
@@ -291,12 +293,12 @@ def tile_picked_ymedu_logs_p_kernel(
         sum_of_exps(1, 0)
         row_bias(0, 1)
         quadrature(1, 0)
-        logp_on_scalar(0, 1)
         row_bias(1, 0)
+        logp_on_scalar(0, 1)
         fetch(0, 0)
         row_max(2, 0)
         row_max(2, 1)
-        logp_on_gpsimd(1, 0)
+        logp_from_copy(1, 0, nc.gpsimd)
         sum_of_exps(1, 1)
         quadrature(1, 1)
         sum_of_exps(2, 0)
@@ -310,7 +312,7 @@ def tile_picked_ymedu_logs_p_kernel(
         logp_on_scalar(2, 1)
 
         fetch(0, 1)
-        logp_on_vector(1, 1)
+        logp_from_copy(1, 1, nc.vector)
         fetch(1, 0)
         fetch(1, 1)
         fetch(2, 0)

@@ -40,7 +40,6 @@ NEG_MAX, SUM, QUAD, BIAS = range(4)
 
 RAW_BYTES = PACK * V * 4
 GROUPED_BYTES = PACK * V * 2
-TERMS_OVERLAP = 128
 
 
 def vanishing_offset():
@@ -81,14 +80,13 @@ def tile_picked_ymedu_logs_p_kernel(
             "stats1_0": raw_at(2, 0) + half_raw,
             "exps0_1": raw_at(2, 1),
             "stats1_1": grouped_at(2, 1),
-            "total0_0_0": grouped_at(2, 1) + GROUPED_BYTES // 2,
             "terms0_0": grouped_at(2, 0),
             "codes2_0": raw_at(2, 1) + half_raw,
-            "logp0_0": grouped_at(1, 1),
-            "logp1_0": grouped_at(1, 1),
-            "terms1_0": raw_at(0, 0) + half_raw - TERMS_OVERLAP,
+            "logp0_0": grouped_at(2, 0),
+            "negated0_0": raw_at(0, 1),
+            "total0_0_0": raw_at(0, 1),
+            "terms1_0": raw_at(0, 0) + half_raw - 128,
             "exps1_1": raw_at(0, 0),
-            "logp0_1": raw_at(0, 0) + half_raw,
         }
 
         def new_tile(shape, dtype, label):
@@ -268,7 +266,7 @@ def tile_picked_ymedu_logs_p_kernel(
         interleave(1, 1, on_vector)
         quantize(1, 0)
         quantize(1, 1)
-        row_max(0, 1)
+        row_max_and_copy(0, 1)
         sum_of_exps(0, 0)
         for g in range(PASSES):
             for m in range(ROW_TILES):
@@ -276,29 +274,28 @@ def tile_picked_ymedu_logs_p_kernel(
 
         quadrature(0, 0)
         row_bias(0, 0)
-        logp_from_copy(0, 0, nc.gpsimd)
         interleave(2, 0, on_scalar)
         interleave(2, 1, on_vector, 0, VECTOR_COLUMNS)
         interleave(2, 1, on_scalar, VECTOR_COLUMNS, V)
         sum_of_exps(0, 1)
-        row_max_and_copy(1, 0)
+        row_max(1, 0)
         for g in reversed(range(PASSES)):
             quantize(2, g)
-        for g in reversed(range(PASSES)):
-            for m in range(ROW_TILES):
+        for m in range(ROW_TILES):
+            for g in reversed(range(PASSES)):
                 multiply(2, m, g)
 
+        logp_from_copy(0, 0, nc.gpsimd)
         row_max_and_copy(1, 1)
+        row_max(2, 0)
+        row_max(2, 1)
         quadrature(0, 1)
         sum_of_exps(1, 0)
         row_bias(0, 1)
+        logp_from_copy(0, 1, nc.gpsimd)
         quadrature(1, 0)
         row_bias(1, 0)
-        logp_on_scalar(0, 1)
-        fetch(0, 0)
-        row_max(2, 0)
-        row_max(2, 1)
-        logp_from_copy(1, 0, nc.gpsimd)
+        logp_on_scalar(1, 0)
         sum_of_exps(1, 1)
         quadrature(1, 1)
         sum_of_exps(2, 0)
@@ -311,6 +308,7 @@ def tile_picked_ymedu_logs_p_kernel(
         row_bias(2, 1)
         logp_on_scalar(2, 1)
 
+        fetch(0, 0)
         fetch(0, 1)
         logp_from_copy(1, 1, nc.vector)
         fetch(1, 0)

@@ -80,7 +80,7 @@ def tile_picked_ymedu_logs_p_kernel(
             "stats1_0": raw_at(2, 0) + half_raw,
             "exps0_1": raw_at(2, 1),
             "stats1_1": grouped_at(2, 1),
-            "terms0_0": grouped_at(2, 0),
+            "terms0_0": raw_at(2, 0),
             "codes2_0": raw_at(2, 1) + half_raw,
             "logp0_0": grouped_at(2, 0),
             "negated0_0": raw_at(0, 1),
@@ -272,17 +272,16 @@ def tile_picked_ymedu_logs_p_kernel(
             for m in range(ROW_TILES):
                 multiply(1, m, g)
 
-        quadrature(0, 0)
-        row_bias(0, 0)
         interleave(2, 0, on_scalar)
-        interleave(2, 1, on_vector, 0, VECTOR_COLUMNS)
-        interleave(2, 1, on_scalar, VECTOR_COLUMNS, V)
+        quadrature(0, 0)
+        interleave(2, 1, on_vector, 0, 160)
+        interleave(2, 1, on_scalar, 160, V)
+        row_bias(0, 0)
         sum_of_exps(0, 1)
         row_max(1, 0)
-        for g in reversed(range(PASSES)):
-            quantize(2, g)
         for m in range(ROW_TILES):
             for g in reversed(range(PASSES)):
+                quantize(2, g, m * P, (m + 1) * P)
                 multiply(2, m, g)
 
         logp_from_copy(0, 0, nc.gpsimd)

@@ -30,6 +30,7 @@ RUN = 2
 LAST_HEAD = HEADS - 1
 
 VECTOR_COLUMNS = 192
+VECTOR_COLUMNS_LAST = 160
 
 NODES = 68
 STEP = 0.42
@@ -40,6 +41,7 @@ NEG_MAX, SUM, QUAD, BIAS = range(4)
 
 RAW_BYTES = PACK * V * 4
 GROUPED_BYTES = PACK * V * 2
+ALIGN = 64
 
 
 def vanishing_offset():
@@ -73,35 +75,35 @@ def tile_picked_ymedu_logs_p_kernel(
         def grouped_at(i, g):
             return raw_at(i, g) + RAW_BYTES
 
-        half_raw = RAW_BYTES // 2
+        quarter_raw = RAW_BYTES // 4
         shared = {
             "stats0_0": raw_at(1, 0),
             "stats0_1": raw_at(1, 1),
-            "stats1_0": raw_at(2, 0) + half_raw,
-            "exps0_1": raw_at(2, 1),
-            "stats1_1": grouped_at(2, 1),
+            "stats1_0": raw_at(2, 0) + 2 * quarter_raw,
             "terms0_0": raw_at(2, 0),
-            "codes2_0": raw_at(2, 1) + half_raw,
-            "logp0_0": grouped_at(2, 0),
+            "exps0_1": raw_at(2, 0) + quarter_raw,
+            "codes2_0": raw_at(2, 1) + 2 * quarter_raw,
+            "stats1_1": grouped_at(2, 1),
+            "logp0_0": grouped_at(2, 1) + ALIGN,
             "negated0_0": raw_at(0, 1),
             "total0_0_0": raw_at(0, 1),
-            "terms1_0": raw_at(0, 0) + half_raw - 128,
+            "terms1_0": raw_at(0, 0),
             "exps1_1": raw_at(0, 0),
         }
 
         def new_tile(shape, dtype, label):
             if label in shared:
-                return staged.tile(shape, dtype, name=label, offset=shared[label], align_bytes=64)
-            return keep.tile(shape, dtype, name=label, align_bytes=64)
+                return staged.tile(shape, dtype, name=label, offset=shared[label], align_bytes=ALIGN)
+            return keep.tile(shape, dtype, name=label, align_bytes=ALIGN)
 
         pairs = [(i, g) for i in range(HEADS) for g in range(PASSES)]
         raw = {
-            (i, g): staged.tile([P, PACK, V], F32, name="raw%d_%d" % (i, g), offset=raw_at(i, g), align_bytes=64)
+            (i, g): staged.tile([P, PACK, V], F32, name="raw%d_%d" % (i, g), offset=raw_at(i, g), align_bytes=ALIGN)
             for i, g in pairs
         }
         grouped = {
             (i, g): staged.tile(
-                [P, V * PACK], BF16, name="grouped%d_%d" % (i, g), offset=grouped_at(i, g), align_bytes=64
+                [P, V * PACK], BF16, name="grouped%d_%d" % (i, g), offset=grouped_at(i, g), align_bytes=ALIGN
             )
             for i, g in pairs
         }
@@ -205,7 +207,7 @@ def tile_picked_ymedu_logs_p_kernel(
             )
 
         def sum_of_exps(i, m):
-            exps = new_tile([P, S], F32, "exps%d_%d" % (i, m))
+            exps = new_tile([P, S], BF16, "exps%d_%d" % (i, m))
             nc.scalar.activation(
                 exps[:], banks[i, m][:], ACT.Exp, bias=column(i, m, NEG_MAX), accum_out=column(i, m, SUM)
             )
@@ -263,21 +265,24 @@ def tile_picked_ymedu_logs_p_kernel(
         interleave(1, 0, on_vector, 0, VECTOR_COLUMNS)
         interleave(1, 0, on_scalar, VECTOR_COLUMNS, V)
         row_max_and_copy(0, 0)
-        interleave(1, 1, on_vector)
         quantize(1, 0)
-        quantize(1, 1)
+        for m in range(ROW_TILES):
+            multiply(1, m, 0)
+        interleave(1, 1, on_vector, 0, P)
+        interleave(1, 1, on_vector, P, VECTOR_COLUMNS)
+        interleave(1, 1, on_scalar, VECTOR_COLUMNS, V)
+        for m in range(ROW_TILES):
+            quantize(1, 1, m * P, (m + 1) * P)
+            multiply(1, m, 1)
         row_max_and_copy(0, 1)
         sum_of_exps(0, 0)
-        for g in range(PASSES):
-            for m in range(ROW_TILES):
-                multiply(1, m, g)
 
         interleave(2, 0, on_scalar)
+        interleave(2, 1, on_vector, 0, VECTOR_COLUMNS_LAST)
+        interleave(2, 1, on_scalar, VECTOR_COLUMNS_LAST, V)
         quadrature(0, 0)
-        interleave(2, 1, on_vector, 0, 160)
-        interleave(2, 1, on_scalar, 160, V)
-        row_bias(0, 0)
         sum_of_exps(0, 1)
+        row_bias(0, 0)
         row_max(1, 0)
         for m in range(ROW_TILES):
             for g in reversed(range(PASSES)):

@@ -24,13 +24,10 @@ PASSES = K // K_PASS
 ROW_TILES = V // P
 QUADRANT = 32
 SCALE_ROWS = 4
-ROW_STEP = QUADRANT // SCALE_ROWS
+ROW_STEP = QUADRANT // (PASSES * SCALE_ROWS)
 LIST_GROUP = 16
 RUN = 2
 LAST_HEAD = HEADS - 1
-
-VECTOR_COLUMNS = 192
-VECTOR_COLUMNS_LAST = 160
 
 NODES = 68
 STEP = 0.42
@@ -39,8 +36,7 @@ HALVINGS = 60
 
 NEG_MAX, SUM, QUAD, BIAS = range(4)
 
-RAW_BYTES = PACK * V * 4
-GROUPED_BYTES = PACK * V * 2
+SLOT = 2048
 ALIGN = 64
 
 
@@ -69,44 +65,25 @@ def tile_picked_ymedu_logs_p_kernel(
         staged = ctx.enter_context(tc.tile_pool(name="staged", bufs=1))
         psum = ctx.enter_context(tc.psum_pool(name="psum", bufs=1))
 
-        def raw_at(i, g):
-            return (PASSES * i + g) * (RAW_BYTES + GROUPED_BYTES)
-
-        def grouped_at(i, g):
-            return raw_at(i, g) + RAW_BYTES
-
-        quarter_raw = RAW_BYTES // 4
-        shared = {
-            "stats0_0": raw_at(1, 0),
-            "stats0_1": raw_at(1, 1),
-            "stats1_0": raw_at(2, 0) + 2 * quarter_raw,
-            "terms0_0": raw_at(2, 0),
-            "exps0_1": raw_at(2, 0) + quarter_raw,
-            "codes2_0": raw_at(2, 1) + 2 * quarter_raw,
-            "stats1_1": grouped_at(2, 1),
-            "logp0_0": grouped_at(2, 1) + ALIGN,
-            "negated0_0": raw_at(0, 1),
-            "total0_0_0": raw_at(0, 1),
-            "terms1_0": raw_at(0, 0),
-            "exps1_1": raw_at(0, 0),
-        }
+        tenants = [
+            {"raw1_0": 0, "stats0_0": 0},
+            {"raw1_1": 0, "stats0_1": 0},
+            {"raw2_0": 0, "terms0_0": 0, "exps0_1": 1024, "stats1_0": 2048},
+            {"raw2_1": 0, "codes2_0": 2048},
+            {"grouped2_1": 0, "stats1_1": 0, "logp0_0": ALIGN},
+            {"raw0_1": 0, "negated0_0": 0, "total0_0_0": 0},
+            {"raw0_0": 0, "terms1_0": 0, "exps1_1": 0},
+        ]
+        place = {label: 2 * SLOT * n + at for n, line in enumerate(tenants) for label, at in line.items()}
 
         def new_tile(shape, dtype, label):
-            if label in shared:
-                return staged.tile(shape, dtype, name=label, offset=shared[label], align_bytes=ALIGN)
+            if label in place:
+                return staged.tile(shape, dtype, name=label, offset=place[label], align_bytes=ALIGN)
             return keep.tile(shape, dtype, name=label, align_bytes=ALIGN)
 
         pairs = [(i, g) for i in range(HEADS) for g in range(PASSES)]
-        raw = {
-            (i, g): staged.tile([P, PACK, V], F32, name="raw%d_%d" % (i, g), offset=raw_at(i, g), align_bytes=ALIGN)
-            for i, g in pairs
-        }
-        grouped = {
-            (i, g): staged.tile(
-                [P, V * PACK], BF16, name="grouped%d_%d" % (i, g), offset=grouped_at(i, g), align_bytes=ALIGN
-            )
-            for i, g in pairs
-        }
+        raw = {(i, g): new_tile([P, PACK, V], F32, "raw%d_%d" % (i, g)) for i, g in pairs}
+        grouped = {(i, g): new_tile([P, V * PACK], BF16, "grouped%d_%d" % (i, g)) for i, g in pairs}
         codes = {(i, g): new_tile([P, V], U32, "codes%d_%d" % (i, g)) for i, g in pairs}
         planes = {(i, g): new_tile([P, V], U8, "planes%d_%d" % (i, g)) for i, g in pairs}
 
@@ -114,46 +91,29 @@ def tile_picked_ymedu_logs_p_kernel(
         tree_offsets = [keep.tile([P, U // LIST_GROUP], U16, name="tree%d" % i) for i in range(HEADS)]
         words = [new_tile([P, T], I32, "words%d" % g) for g in range(PASSES)]
         picked_words = [new_tile([P, S], U32, "picked_words%d" % g) for g in range(PASSES)]
-        scale_rows = new_tile([P, PASSES * T], U8, "scale_rows")
-        picked_rows = new_tile([P, PASSES * S], U8, "picked_rows")
+        scale_rows = new_tile([P, T], U8, "scale_rows")
+        picked_rows = new_tile([P, S], U8, "picked_rows")
         picked_planes = new_tile([P, PASSES * S], U8, "picked_planes")
 
         def load_head(i, g):
             rows = heads[i][g * K_PASS : (g + 1) * K_PASS, :]
             nc.sync.dma_start(out=raw[i, g][:], in_=rows.rearrange("(p j) t -> p j t", j=PACK))
 
-        nc.vector.memset(scale_rows[:, :T].bitcast(I32), 0)
-        nc.gpsimd.memset(scale_rows[:, T:].bitcast(I32), 0)
-        load_head(0, 0)
-        nc.sync.dma_start(offsets[:], offs)
-        nc.sync.dma_start(
-            out=scale_rows[0:P:ROW_STEP, :].bitcast(I32).rearrange("r (g n) -> r g n", g=PASSES),
-            in_=x_scales.bitcast(I32).rearrange("g r n -> r g n"),
-        )
-        for g in range(PASSES):
+        def load_words(g):
             nc.sync.dma_start(out=words[g][:], in_=x_words[g].rearrange("p n b -> p (n b)").bitcast(I32))
-        load_head(0, 1)
 
-        for g in range(PASSES):
-            window = scale_rows[:, g * T : (g + 1) * T]
-            nc.vector.tensor_copy(picked_rows[:, g * S : (g + 1) * S], window.indirect(offsets[:]))
-        nc.vector.tensor_copy(picked_planes[:].bitcast(I32), picked_rows[:].bitcast(I32))
-        for s in range(1, SCALE_ROWS):
+        def load_scale_rows():
             nc.sync.dma_start(
-                out=picked_planes[s:P:QUADRANT, :].bitcast(I32),
-                in_=picked_rows[ROW_STEP * s : P : QUADRANT, :].bitcast(I32),
+                out=scale_rows[0:P:ROW_STEP, :].bitcast(I32),
+                in_=x_scales.bitcast(I32).rearrange("g r n -> r g n"),
             )
 
-        for i in range(1, HEADS):
-            for g in range(PASSES):
-                load_head(i, g)
-        for i in range(HEADS):
-            nc.sync.dma_start(tree_offsets[i][:], trees[i])
-
-        count = keep.tile([P, NODES], F32, name="count")
-        nc.gpsimd.iota(count[:], [[1, NODES]], base=0, channel_multiplier=0, allow_small_or_imprecise_dtypes=True)
-        nodes = keep.tile([P, NODES], F32, name="nodes")
-        nc.scalar.activation(nodes[:], count[:], ACT.Exp, scale=STEP, bias=FIRST)
+        def move_planes(q):
+            first = QUADRANT * q
+            nc.sync.dma_start(
+                out=picked_planes[first : first + SCALE_ROWS, :].bitcast(I32),
+                in_=picked_rows[first : first + QUADRANT : ROW_STEP, :].bitcast(I32),
+            )
 
         on_vector = nc.vector.tensor_copy
         on_scalar = nc.scalar.copy
@@ -236,13 +196,17 @@ def tile_picked_ymedu_logs_p_kernel(
             logp[i, m] = new_tile([P, S], F32, "logp%d_%d" % (i, m))
             engine.tensor_scalar(logp[i, m][:], negated[i, m][:], -1.0, column(i, m, BIAS), ALU.mult, ALU.add)
 
+        def fetch_on_scalar(i, m):
+            total[m] = new_tile([P, U], F32, "total%d_%d_0" % (i, m))
+            nc.scalar.activation(total[m][:], logp[i, m][:].indirect(tree_offsets[i][:]), ACT.Copy)
+
         def fetch(i, m, pieces=1):
             width = U // pieces
             for c in range(pieces):
                 acc = new_tile([P, width], F32, "total%d_%d_%d" % (i, m, c))
                 cols = slice(c * width, (c + 1) * width)
                 entries = tree_offsets[i][:, c * width // LIST_GROUP : (c + 1) * width // LIST_GROUP]
-                if i == 0:
+                if m not in total:
                     nc.vector.tensor_copy(acc[:], logp[i, m][:].indirect(entries))
                 else:
                     nc.vector.tensor_tensor(acc[:], logp[i, m][:].indirect(entries), total[m][:, cols], ALU.add)
@@ -250,27 +214,53 @@ def tile_picked_ymedu_logs_p_kernel(
                     nc.sync.dma_start(out=out[m * P : (m + 1) * P, cols], in_=acc[:])
             total[m] = acc
 
+        def row_tile(m):
+            return m * P, (m + 1) * P
+
+        nc.vector.memset(scale_rows[:].bitcast(I32), 0)
+        nc.gpsimd.memset(picked_planes[:].bitcast(I32), 0)
+        load_head(0, 0)
+        nc.sync.dma_start(offsets[:], offs)
+        load_scale_rows()
+        for g in range(PASSES):
+            load_words(g)
+        nc.vector.tensor_copy(picked_rows[:], scale_rows[:].indirect(offsets[:]))
+        for q in range(P // QUADRANT):
+            move_planes(q)
+        load_head(0, 1)
+        for i in range(1, HEADS):
+            for g in range(PASSES):
+                load_head(i, g)
+        for i in range(HEADS):
+            nc.sync.dma_start(tree_offsets[i][:], trees[i])
+
+        count = keep.tile([P, NODES], F32, name="count")
+        nc.gpsimd.iota(count[:], [[1, NODES]], base=0, channel_multiplier=0, allow_small_or_imprecise_dtypes=True)
+        nodes = keep.tile([P, NODES], F32, name="nodes")
+        nc.scalar.activation(nodes[:], count[:], ACT.Exp, scale=STEP, bias=FIRST)
+
         interleave(0, 0, on_scalar)
         quantize(0, 0)
         for g in range(PASSES):
             nc.vector.tensor_copy(picked_words[g][:], words[g][:].bitcast(U32).indirect(offsets[:]))
         for m in range(ROW_TILES):
+            multiply(0, m, 0)
+        for m in range(ROW_TILES):
             interleave(0, 1, on_vector, m * P, m * P + P // 2)
             interleave(0, 1, on_scalar, m * P + P // 2, (m + 1) * P)
         for m in range(ROW_TILES):
-            quantize(0, 1, m * P, (m + 1) * P)
-            for g in range(PASSES):
-                multiply(0, m, g)
+            quantize(0, 1, *row_tile(m))
+            multiply(0, m, 1)
 
-        interleave(1, 0, on_vector, 0, VECTOR_COLUMNS)
-        interleave(1, 0, on_scalar, VECTOR_COLUMNS, V)
+        interleave(1, 0, on_vector, 0, 192)
+        interleave(1, 0, on_scalar, 192, V)
         row_max_and_copy(0, 0)
         quantize(1, 0)
         for m in range(ROW_TILES):
             multiply(1, m, 0)
         interleave(1, 1, on_vector, 0, P)
-        interleave(1, 1, on_vector, P, VECTOR_COLUMNS)
-        interleave(1, 1, on_scalar, VECTOR_COLUMNS, V)
+        interleave(1, 1, on_vector, P, 192)
+        interleave(1, 1, on_scalar, 192, V)
         for m in range(ROW_TILES):
             quantize(1, 1, m * P, (m + 1) * P)
             multiply(1, m, 1)
@@ -278,8 +268,8 @@ def tile_picked_ymedu_logs_p_kernel(
         sum_of_exps(0, 0)
 
         interleave(2, 0, on_scalar)
-        interleave(2, 1, on_vector, 0, VECTOR_COLUMNS_LAST)
-        interleave(2, 1, on_scalar, VECTOR_COLUMNS_LAST, V)
+        interleave(2, 1, on_vector, 0, 160)
+        interleave(2, 1, on_scalar, 160, V)
         quadrature(0, 0)
         sum_of_exps(0, 1)
         row_bias(0, 0)

@@ -66,13 +66,13 @@ def tile_picked_ymedu_logs_p_kernel(
         psum = ctx.enter_context(tc.psum_pool(name="psum", bufs=1))
 
         tenants = [
-            {"raw1_0": 0, "stats0_0": 0},
+            {"raw0_1_1": 0, "stats0_0": 0},
             {"raw1_1": 0, "stats0_1": 0},
-            {"raw2_0": 0, "terms0_0": 0, "exps0_1": 1024, "stats1_0": 2048},
-            {"raw2_1": 0, "codes2_0": 2048},
-            {"grouped2_1": 0, "stats1_1": 0, "logp0_0": ALIGN},
-            {"raw0_1": 0, "negated0_0": 0, "total0_0_0": 0},
-            {"raw0_0": 0, "terms1_0": 0, "exps1_1": 0},
+            {"grouped1_1": 0, "logp0_0": 0},
+            {"raw2_1": 0, "codes2_0": 0},
+            {"grouped2_0": 0, "stats1_1": 0, "logp0_1": ALIGN},
+            {"negated1_0": 0, "total0_1_0": 0},
+            {"terms1_0": 896, "total0_0_0": 0, "exps1_1": 1024},
         ]
         place = {label: 2 * SLOT * n + at for n, line in enumerate(tenants) for label, at in line.items()}
 
@@ -82,7 +82,10 @@ def tile_picked_ymedu_logs_p_kernel(
             return keep.tile(shape, dtype, name=label, align_bytes=ALIGN)
 
         pairs = [(i, g) for i in range(HEADS) for g in range(PASSES)]
-        raw = {(i, g): new_tile([P, PACK, V], F32, "raw%d_%d" % (i, g)) for i, g in pairs}
+        raw = {(i, g): new_tile([P, PACK, V], F32, "raw%d_%d" % (i, g)) for i, g in pairs if i > 0}
+        raw_first = {
+            (g, m): new_tile([P, PACK, P], F32, "raw0_%d_%d" % (g, m)) for g in range(PASSES) for m in range(ROW_TILES)
+        }
         grouped = {(i, g): new_tile([P, V * PACK], BF16, "grouped%d_%d" % (i, g)) for i, g in pairs}
         codes = {(i, g): new_tile([P, V], U32, "codes%d_%d" % (i, g)) for i, g in pairs}
         planes = {(i, g): new_tile([P, V], U8, "planes%d_%d" % (i, g)) for i, g in pairs}
@@ -98,6 +101,10 @@ def tile_picked_ymedu_logs_p_kernel(
         def load_head(i, g):
             rows = heads[i][g * K_PASS : (g + 1) * K_PASS, :]
             nc.sync.dma_start(out=raw[i, g][:], in_=rows.rearrange("(p j) t -> p j t", j=PACK))
+
+        def load_first_head(g, m):
+            rows = h0[g * K_PASS : (g + 1) * K_PASS, m * P : (m + 1) * P]
+            nc.sync.dma_start(out=raw_first[g, m][:], in_=rows.rearrange("(p j) t -> p j t", j=PACK))
 
         def load_words(g):
             nc.sync.dma_start(out=words[g][:], in_=x_words[g].rearrange("p n b -> p (n b)").bitcast(I32))
@@ -119,9 +126,10 @@ def tile_picked_ymedu_logs_p_kernel(
         on_scalar = nc.scalar.copy
 
         def interleave(i, g, copy, lo=0, hi=V):
+            source = raw[i, g][:, :, lo:hi] if i > 0 else raw_first[g, lo // P][:]
             copy(
                 grouped[i, g][:, PACK * lo : PACK * hi].rearrange("p (c n j) -> p c j n", n=RUN, j=PACK),
-                raw[i, g][:, :, lo:hi].rearrange("p j (c n) -> p c j n", n=RUN),
+                source.rearrange("p j (c n) -> p c j n", n=RUN),
             )
 
         def quantize(i, g, lo=0, hi=V):
@@ -219,7 +227,8 @@ def tile_picked_ymedu_logs_p_kernel(
 
         nc.vector.memset(scale_rows[:].bitcast(I32), 0)
         nc.gpsimd.memset(picked_planes[:].bitcast(I32), 0)
-        load_head(0, 0)
+        for g in range(PASSES):
+            load_first_head(g, 0)
         nc.sync.dma_start(offsets[:], offs)
         load_scale_rows()
         for g in range(PASSES):
@@ -227,7 +236,8 @@ def tile_picked_ymedu_logs_p_kernel(
         nc.vector.tensor_copy(picked_rows[:], scale_rows[:].indirect(offsets[:]))
         for q in range(P // QUADRANT):
             move_planes(q)
-        load_head(0, 1)
+        for g in range(PASSES):
+            load_first_head(g, 1)
         for i in range(1, HEADS):
             for g in range(PASSES):
                 load_head(i, g)
@@ -239,57 +249,54 @@ def tile_picked_ymedu_logs_p_kernel(
         nodes = keep.tile([P, NODES], F32, name="nodes")
         nc.scalar.activation(nodes[:], count[:], ACT.Exp, scale=STEP, bias=FIRST)
 
-        interleave(0, 0, on_scalar)
-        quantize(0, 0)
+        for g in range(PASSES):
+            interleave(0, g, on_scalar, *row_tile(0))
+            quantize(0, g, *row_tile(0))
         for g in range(PASSES):
             nc.vector.tensor_copy(picked_words[g][:], words[g][:].bitcast(U32).indirect(offsets[:]))
-        for m in range(ROW_TILES):
-            multiply(0, m, 0)
-        for m in range(ROW_TILES):
-            interleave(0, 1, on_vector, m * P, m * P + P // 2)
-            interleave(0, 1, on_scalar, m * P + P // 2, (m + 1) * P)
-        for m in range(ROW_TILES):
-            quantize(0, 1, *row_tile(m))
-            multiply(0, m, 1)
+            multiply(0, 0, g)
+        interleave(0, 0, on_scalar, *row_tile(1))
+        interleave(0, 1, on_vector, *row_tile(1))
+        for g in range(PASSES):
+            quantize(0, g, *row_tile(1))
+            multiply(0, 1, g)
 
-        interleave(1, 0, on_vector, 0, 192)
-        interleave(1, 0, on_scalar, 192, V)
         row_max_and_copy(0, 0)
-        quantize(1, 0)
-        for m in range(ROW_TILES):
+        interleave(1, 0, on_vector, *row_tile(0))
+        interleave(1, 0, on_scalar, *row_tile(1))
+        sum_of_exps(0, 0)
+        for m in reversed(range(ROW_TILES)):
+            quantize(1, 0, *row_tile(m))
             multiply(1, m, 0)
         interleave(1, 1, on_vector, 0, P)
         interleave(1, 1, on_vector, P, 192)
         interleave(1, 1, on_scalar, 192, V)
         for m in range(ROW_TILES):
-            quantize(1, 1, m * P, (m + 1) * P)
+            quantize(1, 1, *row_tile(m))
             multiply(1, m, 1)
-        row_max_and_copy(0, 1)
-        sum_of_exps(0, 0)
-
-        interleave(2, 0, on_scalar)
-        interleave(2, 1, on_vector, 0, 160)
-        interleave(2, 1, on_scalar, 160, V)
         quadrature(0, 0)
-        sum_of_exps(0, 1)
         row_bias(0, 0)
-        row_max(1, 0)
-        for m in range(ROW_TILES):
-            for g in reversed(range(PASSES)):
-                quantize(2, g, m * P, (m + 1) * P)
-                multiply(2, m, g)
-
+        row_max_and_copy(0, 1)
+        row_max_and_copy(1, 0)
         logp_from_copy(0, 0, nc.gpsimd)
+        interleave(2, 0, on_scalar)
+        sum_of_exps(0, 1)
+        interleave(2, 1, on_vector)
+        for m in range(ROW_TILES):
+            for g in range(PASSES):
+                quantize(2, g, *row_tile(m))
+                multiply(2, m, g)
+        quadrature(0, 1)
+        row_bias(0, 1)
+        logp_from_copy(0, 1, nc.gpsimd)
         row_max_and_copy(1, 1)
         row_max(2, 0)
         row_max(2, 1)
-        quadrature(0, 1)
         sum_of_exps(1, 0)
-        row_bias(0, 1)
-        logp_from_copy(0, 1, nc.gpsimd)
         quadrature(1, 0)
         row_bias(1, 0)
-        logp_on_scalar(1, 0)
+        logp_from_copy(1, 0, nc.gpsimd)
+        fetch_on_scalar(0, 0)
         sum_of_exps(1, 1)
         quadrature(1, 1)
         sum_of_exps(2, 0)
@@ -301,11 +308,9 @@ def tile_picked_ymedu_logs_p_kernel(
         logp_on_scalar(2, 0)
         row_bias(2, 1)
         logp_on_scalar(2, 1)
-
-        fetch(0, 0)
         fetch(0, 1)
-        logp_from_copy(1, 1, nc.vector)
         fetch(1, 0)
+        logp_from_copy(1, 1, nc.vector)
         fetch(1, 1)
         fetch(2, 0)
         fetch(2, 1, pieces=2)

@@ -69,8 +69,9 @@ def tile_picked_ymedu_logs_p_kernel(
             {"raw0_1_1": 0, "stats0_0": 0},
             {"raw1_1": 0, "stats0_1": 0},
             {"grouped1_1": 0, "logp0_0": 0},
-            {"raw2_1": 0, "codes2_0": 0},
-            {"grouped2_0": 0, "stats1_1": 0, "logp0_1": ALIGN},
+            {"negated0_0": 0, "codes2_0": 0},
+            {"raw2_1": 0, "stats1_1": 0},
+            {"grouped2_1": 0, "logp0_1": 0},
             {"negated1_0": 0, "total0_1_0": 0},
             {"terms1_0": 896, "total0_0_0": 0, "exps1_1": 1024},
         ]
@@ -281,11 +282,14 @@ def tile_picked_ymedu_logs_p_kernel(
         logp_from_copy(0, 0, nc.gpsimd)
         interleave(2, 0, on_scalar)
         sum_of_exps(0, 1)
-        interleave(2, 1, on_vector)
+        quantize(2, 0)
         for m in range(ROW_TILES):
-            for g in range(PASSES):
-                quantize(2, g, *row_tile(m))
-                multiply(2, m, g)
+            multiply(2, m, 0)
+        for m in range(ROW_TILES):
+            interleave(2, 1, on_vector, *row_tile(m))
+        for m in range(ROW_TILES):
+            quantize(2, 1, *row_tile(m))
+            multiply(2, m, 1)
         quadrature(0, 1)
         row_bias(0, 1)
         logp_from_copy(0, 1, nc.gpsimd)
@@ -298,13 +302,13 @@ def tile_picked_ymedu_logs_p_kernel(
         logp_from_copy(1, 0, nc.gpsimd)
         fetch_on_scalar(0, 0)
         sum_of_exps(1, 1)
-        quadrature(1, 1)
         sum_of_exps(2, 0)
+        quadrature(1, 1)
+        sum_of_exps(2, 1)
         row_bias(1, 1)
         quadrature(2, 0)
-        sum_of_exps(2, 1)
-        row_bias(2, 0)
         quadrature(2, 1)
+        row_bias(2, 0)
         logp_on_scalar(2, 0)
         row_bias(2, 1)
         logp_on_scalar(2, 1)

@@ -66,10 +66,11 @@ def tile_picked_ymedu_logs_p_kernel(
         psum = ctx.enter_context(tc.psum_pool(name="psum", bufs=1))
 
         tenants = [
-            {"raw0_1_1": 0, "stats0_0": 0},
+            {"raw1_0": 0, "stats0_0": 0},
             {"raw1_1": 0, "stats0_1": 0},
             {"grouped1_1": 0, "logp0_0": 0},
             {"negated0_0": 0, "codes2_0": 0},
+            {"terms0_0": 0, "grouped2_0": 0},
             {"raw2_1": 0, "stats1_1": 0},
             {"grouped2_1": 0, "logp0_1": 0},
             {"negated1_0": 0, "total0_1_0": 0},
@@ -83,10 +84,7 @@ def tile_picked_ymedu_logs_p_kernel(
             return keep.tile(shape, dtype, name=label, align_bytes=ALIGN)
 
         pairs = [(i, g) for i in range(HEADS) for g in range(PASSES)]
-        raw = {(i, g): new_tile([P, PACK, V], F32, "raw%d_%d" % (i, g)) for i, g in pairs if i > 0}
-        raw_first = {
-            (g, m): new_tile([P, PACK, P], F32, "raw0_%d_%d" % (g, m)) for g in range(PASSES) for m in range(ROW_TILES)
-        }
+        raw = {(i, g): new_tile([P, PACK, V], F32, "raw%d_%d" % (i, g)) for i, g in pairs}
         grouped = {(i, g): new_tile([P, V * PACK], BF16, "grouped%d_%d" % (i, g)) for i, g in pairs}
         codes = {(i, g): new_tile([P, V], U32, "codes%d_%d" % (i, g)) for i, g in pairs}
         planes = {(i, g): new_tile([P, V], U8, "planes%d_%d" % (i, g)) for i, g in pairs}
@@ -102,10 +100,6 @@ def tile_picked_ymedu_logs_p_kernel(
         def load_head(i, g):
             rows = heads[i][g * K_PASS : (g + 1) * K_PASS, :]
             nc.sync.dma_start(out=raw[i, g][:], in_=rows.rearrange("(p j) t -> p j t", j=PACK))
-
-        def load_first_head(g, m):
-            rows = h0[g * K_PASS : (g + 1) * K_PASS, m * P : (m + 1) * P]
-            nc.sync.dma_start(out=raw_first[g, m][:], in_=rows.rearrange("(p j) t -> p j t", j=PACK))
 
         def load_words(g):
             nc.sync.dma_start(out=words[g][:], in_=x_words[g].rearrange("p n b -> p (n b)").bitcast(I32))
@@ -127,10 +121,9 @@ def tile_picked_ymedu_logs_p_kernel(
         on_scalar = nc.scalar.copy
 
         def interleave(i, g, copy, lo=0, hi=V):
-            source = raw[i, g][:, :, lo:hi] if i > 0 else raw_first[g, lo // P][:]
             copy(
                 grouped[i, g][:, PACK * lo : PACK * hi].rearrange("p (c n j) -> p c j n", n=RUN, j=PACK),
-                source.rearrange("p j (c n) -> p c j n", n=RUN),
+                raw[i, g][:, :, lo:hi].rearrange("p j (c n) -> p c j n", n=RUN),
             )
 
         def quantize(i, g, lo=0, hi=V):
@@ -228,8 +221,7 @@ def tile_picked_ymedu_logs_p_kernel(
 
         nc.vector.memset(scale_rows[:].bitcast(I32), 0)
         nc.gpsimd.memset(picked_planes[:].bitcast(I32), 0)
-        for g in range(PASSES):
-            load_first_head(g, 0)
+        load_head(0, 0)
         nc.sync.dma_start(offsets[:], offs)
         load_scale_rows()
         for g in range(PASSES):
@@ -237,8 +229,7 @@ def tile_picked_ymedu_logs_p_kernel(
         nc.vector.tensor_copy(picked_rows[:], scale_rows[:].indirect(offsets[:]))
         for q in range(P // QUADRANT):
             move_planes(q)
-        for g in range(PASSES):
-            load_first_head(g, 1)
+        load_head(0, 1)
         for i in range(1, HEADS):
             for g in range(PASSES):
                 load_head(i, g)
@@ -250,24 +241,24 @@ def tile_picked_ymedu_logs_p_kernel(
         nodes = keep.tile([P, NODES], F32, name="nodes")
         nc.scalar.activation(nodes[:], count[:], ACT.Exp, scale=STEP, bias=FIRST)
 
-        for g in range(PASSES):
-            interleave(0, g, on_scalar, *row_tile(0))
-            quantize(0, g, *row_tile(0))
+        interleave(0, 0, on_scalar)
+        quantize(0, 0)
         for g in range(PASSES):
             nc.vector.tensor_copy(picked_words[g][:], words[g][:].bitcast(U32).indirect(offsets[:]))
-            multiply(0, 0, g)
-        interleave(0, 0, on_scalar, *row_tile(1))
-        interleave(0, 1, on_vector, *row_tile(1))
-        for g in range(PASSES):
-            quantize(0, g, *row_tile(1))
-            multiply(0, 1, g)
+        for m in range(ROW_TILES):
+            multiply(0, m, 0)
+        for m in range(ROW_TILES):
+            interleave(0, 1, on_vector, m * P, m * P + P // 2)
+            interleave(0, 1, on_scalar, m * P + P // 2, (m + 1) * P)
+        for m in range(ROW_TILES):
+            quantize(0, 1, *row_tile(m))
+            multiply(0, m, 1)
 
+        interleave(1, 0, on_vector, 0, 192)
+        interleave(1, 0, on_scalar, 192, V)
         row_max_and_copy(0, 0)
-        interleave(1, 0, on_vector, *row_tile(0))
-        interleave(1, 0, on_scalar, *row_tile(1))
-        sum_of_exps(0, 0)
-        for m in reversed(range(ROW_TILES)):
-            quantize(1, 0, *row_tile(m))
+        quantize(1, 0)
+        for m in range(ROW_TILES):
             multiply(1, m, 0)
         interleave(1, 1, on_vector, 0, P)
         interleave(1, 1, on_vector, P, 192)
@@ -275,6 +266,7 @@ def tile_picked_ymedu_logs_p_kernel(
         for m in range(ROW_TILES):
             quantize(1, 1, *row_tile(m))
             multiply(1, m, 1)
+        sum_of_exps(0, 0)
         quadrature(0, 0)
         row_bias(0, 0)
         row_max_and_copy(0, 1)
@@ -282,11 +274,11 @@ def tile_picked_ymedu_logs_p_kernel(
         logp_from_copy(0, 0, nc.gpsimd)
         interleave(2, 0, on_scalar)
         sum_of_exps(0, 1)
+        interleave(2, 1, on_vector, *row_tile(0))
         quantize(2, 0)
         for m in range(ROW_TILES):
             multiply(2, m, 0)
-        for m in range(ROW_TILES):
-            interleave(2, 1, on_vector, *row_tile(m))
+        interleave(2, 1, on_vector, *row_tile(1))
         for m in range(ROW_TILES):
             quantize(2, 1, *row_tile(m))
             multiply(2, m, 1)

import math
from contextlib import ExitStack

import concourse.mybir as mybir

K, T, S, V, U = 1024, 2048, 512, 256, 256
HEADS = 3
FLOPS = 2 * HEADS * K * V * S

F32 = mybir.dt.float32
BF16 = mybir.dt.bfloat16
I32 = mybir.dt.int32
U32 = mybir.dt.uint32
U16 = mybir.dt.uint16
U8 = mybir.dt.uint8
FP8X4 = mybir.dt.float8_e4m3fn_x4
ACT = mybir.ActivationFunctionType
ALU = mybir.AluOpType

P = 128
PACK = 4
K_PASS = P * PACK
PASSES = K // K_PASS
ROW_TILES = V // P
QUADRANT = 32
SCALE_ROWS = 4
ROW_STEP = QUADRANT // (PASSES * SCALE_ROWS)
LIST_GROUP = 16
RUN = 2
LAST_HEAD = HEADS - 1

NODES = 68
STEP = 0.42
FIRST = -25.8
HALVINGS = 60

NEG_MAX, SUM, QUAD, BIAS = range(4)

SLOT = 2048
ALIGN = 64


def vanishing_offset():
    low, high = 0.0, 1.0
    for halving in range(HALVINGS):
        middle = (low + high) / 2
        if sum(math.tanh(math.e ** (FIRST + STEP * n) - middle) for n in range(NODES)) > 0:
            low = middle
        else:
            high = middle
    return (low + high) / 2


def tile_picked_ymedu_logs_p_kernel(
    tc, x_words, x_scales, h0, h1, h2, offs, tree1, tree2, tree3, out
):
    nc = tc.nc
    heads = (h0, h1, h2)
    trees = (tree1, tree2, tree3)
    tanh_offset = vanishing_offset()
    log_factor = STEP / (1 + math.tanh(tanh_offset))

    with ExitStack() as ctx:
        keep = ctx.enter_context(tc.tile_pool(name="keep", bufs=1))
        staged = ctx.enter_context(tc.tile_pool(name="staged", bufs=1))
        psum = ctx.enter_context(tc.psum_pool(name="psum", bufs=1))

        tenants = [
            {"raw1_0": 0, "stats0_0": 0},
            {"raw1_1": 0, "stats0_1": 0},
            {"grouped1_1": 0, "logp0_0": 0},
            {"negated0_0": 0, "codes2_0": 0},
            {"terms0_0": 0, "grouped2_0": 0},
            {"raw2_1": 0, "stats1_1": 0},
            {"grouped2_1": 0, "logp0_1": 0},
            {"negated1_0": 0, "total0_1_0": 0},
            {"terms1_0": 896, "total0_0_0": 0, "exps1_1": 1024},
        ]
        place = {label: 2 * SLOT * n + at for n, line in enumerate(tenants) for label, at in line.items()}

        def new_tile(shape, dtype, label):
            if label in place:
                return staged.tile(shape, dtype, name=label, offset=place[label], align_bytes=ALIGN)
            return keep.tile(shape, dtype, name=label, align_bytes=ALIGN)

        pairs = [(i, g) for i in range(HEADS) for g in range(PASSES)]
        raw = {(i, g): new_tile([P, PACK, V], F32, "raw%d_%d" % (i, g)) for i, g in pairs}
        grouped = {(i, g): new_tile([P, V * PACK], BF16, "grouped%d_%d" % (i, g)) for i, g in pairs}
        codes = {(i, g): new_tile([P, V], U32, "codes%d_%d" % (i, g)) for i, g in pairs}
        planes = {(i, g): new_tile([P, V], U8, "planes%d_%d" % (i, g)) for i, g in pairs}

        offsets = keep.tile([P, S // LIST_GROUP], U16, name="offsets")
        tree_offsets = [keep.tile([P, U // LIST_GROUP], U16, name="tree%d" % i) for i in range(HEADS)]
        words = [new_tile([P, T], I32, "words%d" % g) for g in range(PASSES)]
        picked_words = [new_tile([P, S], U32, "picked_words%d" % g) for g in range(PASSES)]
        scale_rows = new_tile([P, T], U8, "scale_rows")
        picked_rows = new_tile([P, S], U8, "picked_rows")
        picked_planes = new_tile([P, PASSES * S], U8, "picked_planes")

        def load_head(i, g):
            rows = heads[i][g * K_PASS : (g + 1) * K_PASS, :]
            nc.sync.dma_start(out=raw[i, g][:], in_=rows.rearrange("(p j) t -> p j t", j=PACK))

        def load_words(g):
            nc.sync.dma_start(out=words[g][:], in_=x_words[g].rearrange("p n b -> p (n b)").bitcast(I32))

        def load_scale_rows():
            nc.sync.dma_start(
                out=scale_rows[0:P:ROW_STEP, :].bitcast(I32),
                in_=x_scales.bitcast(I32).rearrange("g r n -> r g n"),
            )

        def move_planes(q):
            first = QUADRANT * q
            nc.sync.dma_start(
                out=picked_planes[first : first + SCALE_ROWS, :].bitcast(I32),
                in_=picked_rows[first : first + QUADRANT : ROW_STEP, :].bitcast(I32),
            )

        on_vector = nc.vector.tensor_copy
        on_scalar = nc.scalar.copy

        def interleave(i, g, copy, lo=0, hi=V):
            copy(
                grouped[i, g][:, PACK * lo : PACK * hi].rearrange("p (c n j) -> p c j n", n=RUN, j=PACK),
                raw[i, g][:, :, lo:hi].rearrange("p j (c n) -> p c j n", n=RUN),
            )

        def quantize(i, g, lo=0, hi=V):
            nc.vector.quantize_mx(
                out=codes[i, g][:, lo:hi].bitcast(FP8X4),
                scales=planes[i, g][:, lo:hi],
                in_=grouped[i, g][:, PACK * lo : PACK * hi],
            )

        banks = {}
        stats = {}
        negated = {}
        logp = {}
        total = {}

        def multiply(i, m, g):
            first = (i, m) not in banks
            if first:
                banks[i, m] = psum.tile([P, S], F32, name="bank%d_%d" % (i, m))
            cols = slice(m * P, (m + 1) * P)
            nc.tensor.matmul_mx(
                out=banks[i, m][:],
                lhsT=codes[i, g][:, cols].bitcast(FP8X4),
                lhsT_scale=planes[i, g][:, cols],
                rhs=picked_words[g][:].bitcast(FP8X4),
                rhs_scale=picked_planes[:, g * S : (g + 1) * S],
                start=first,
                stop=not first,
            )

        def column(i, m, c):
            return stats[i, m][:, c : c + 1]

        def row_max(i, m):
            stats[i, m] = new_tile([P, 4], F32, "stats%d_%d" % (i, m))
            nc.vector.tensor_reduce(column(i, m, NEG_MAX), banks[i, m][:], mybir.AxisListType.X, ALU.max, negate=True)

        def row_max_and_copy(i, m):
            stats[i, m] = new_tile([P, 4], F32, "stats%d_%d" % (i, m))
            negated[i, m] = new_tile([P, S], F32, "negated%d_%d" % (i, m))
            nc.vector.tensor_scalar(
                negated[i, m][:], banks[i, m][:], -1.0, None, ALU.mult, ALU.min, accum_out=column(i, m, NEG_MAX)
            )

        def sum_of_exps(i, m):
            exps = new_tile([P, S], BF16, "exps%d_%d" % (i, m))
            nc.scalar.activation(
                exps[:], banks[i, m][:], ACT.Exp, bias=column(i, m, NEG_MAX), accum_out=column(i, m, SUM)
            )

        def quadrature(i, m):
            terms = new_tile([P, NODES], F32, "terms%d_%d" % (i, m))
            nc.scalar.activation(
                terms[:],
                nodes[:],
                ACT.Tanh,
                scale=column(i, m, SUM),
                bias=-tanh_offset,
                accum_out=column(i, m, QUAD),
            )

        def row_bias(i, m):
            nc.scalar.activation(
                column(i, m, BIAS), column(i, m, QUAD), ACT.Identity, scale=-log_factor, bias=column(i, m, NEG_MAX)
            )

        def logp_on_scalar(i, m):
            logp[i, m] = new_tile([P, S], F32, "logp%d_%d" % (i, m))
            nc.scalar.activation(logp[i, m][:], banks[i, m][:], ACT.Identity, bias=column(i, m, BIAS))

        def logp_from_copy(i, m, engine):
            logp[i, m] = new_tile([P, S], F32, "logp%d_%d" % (i, m))
            engine.tensor_scalar(logp[i, m][:], negated[i, m][:], -1.0, column(i, m, BIAS), ALU.mult, ALU.add)

        def fetch_on_scalar(i, m):
            total[m] = new_tile([P, U], F32, "total%d_%d_0" % (i, m))
            nc.scalar.activation(total[m][:], logp[i, m][:].indirect(tree_offsets[i][:]), ACT.Copy)

        def fetch(i, m, pieces=1):
            width = U // pieces
            for c in range(pieces):
                acc = new_tile([P, width], F32, "total%d_%d_%d" % (i, m, c))
                cols = slice(c * width, (c + 1) * width)
                entries = tree_offsets[i][:, c * width // LIST_GROUP : (c + 1) * width // LIST_GROUP]
                if m not in total:
                    nc.vector.tensor_copy(acc[:], logp[i, m][:].indirect(entries))
                else:
                    nc.vector.tensor_tensor(acc[:], logp[i, m][:].indirect(entries), total[m][:, cols], ALU.add)
                if i == LAST_HEAD:
                    nc.sync.dma_start(out=out[m * P : (m + 1) * P, cols], in_=acc[:])
            total[m] = acc

        def row_tile(m):
            return m * P, (m + 1) * P

        nc.vector.memset(scale_rows[:].bitcast(I32), 0)
        nc.gpsimd.memset(picked_planes[:].bitcast(I32), 0)
        load_head(0, 0)
        nc.sync.dma_start(offsets[:], offs)
        load_scale_rows()
        for g in range(PASSES):
            load_words(g)
        nc.vector.tensor_copy(picked_rows[:], scale_rows[:].indirect(offsets[:]))
        for q in range(P // QUADRANT):
            move_planes(q)
        load_head(0, 1)
        for i in range(1, HEADS):
            for g in range(PASSES):
                load_head(i, g)
        for i in range(HEADS):
            nc.sync.dma_start(tree_offsets[i][:], trees[i])

        count = keep.tile([P, NODES], F32, name="count")
        nc.gpsimd.iota(count[:], [[1, NODES]], base=0, channel_multiplier=0, allow_small_or_imprecise_dtypes=True)
        nodes = keep.tile([P, NODES], F32, name="nodes")
        nc.scalar.activation(nodes[:], count[:], ACT.Exp, scale=STEP, bias=FIRST)

        interleave(0, 0, on_scalar)
        quantize(0, 0)
        for g in range(PASSES):
            nc.vector.tensor_copy(picked_words[g][:], words[g][:].bitcast(U32).indirect(offsets[:]))
        for m in range(ROW_TILES):
            multiply(0, m, 0)
        for m in range(ROW_TILES):
            interleave(0, 1, on_vector, m * P, m * P + P // 2)
            interleave(0, 1, on_scalar, m * P + P // 2, (m + 1) * P)
        for m in range(ROW_TILES):
            quantize(0, 1, *row_tile(m))
            multiply(0, m, 1)

        interleave(1, 0, on_vector, 0, 192)
        interleave(1, 0, on_scalar, 192, V)
        row_max_and_copy(0, 0)
        quantize(1, 0)
        for m in range(ROW_TILES):
            multiply(1, m, 0)
        interleave(1, 1, on_vector, 0, P)
        interleave(1, 1, on_vector, P, 192)
        interleave(1, 1, on_scalar, 192, V)
        for m in range(ROW_TILES):
            quantize(1, 1, *row_tile(m))
            multiply(1, m, 1)
        sum_of_exps(0, 0)
        quadrature(0, 0)
        row_bias(0, 0)
        row_max_and_copy(0, 1)
        row_max_and_copy(1, 0)
        logp_from_copy(0, 0, nc.gpsimd)
        interleave(2, 0, on_scalar)
        sum_of_exps(0, 1)
        interleave(2, 1, on_vector, *row_tile(0))
        quantize(2, 0)
        for m in range(ROW_TILES):
            multiply(2, m, 0)
        interleave(2, 1, on_vector, *row_tile(1))
        for m in range(ROW_TILES):
            quantize(2, 1, *row_tile(m))
            multiply(2, m, 1)
        quadrature(0, 1)
        row_bias(0, 1)
        logp_from_copy(0, 1, nc.gpsimd)
        row_max_and_copy(1, 1)
        row_max(2, 0)
        row_max(2, 1)
        sum_of_exps(1, 0)
        quadrature(1, 0)
        row_bias(1, 0)
        logp_from_copy(1, 0, nc.gpsimd)
        fetch_on_scalar(0, 0)
        sum_of_exps(1, 1)
        sum_of_exps(2, 0)
        quadrature(1, 1)
        sum_of_exps(2, 1)
        row_bias(1, 1)
        quadrature(2, 0)
        quadrature(2, 1)
        row_bias(2, 0)
        logp_on_scalar(2, 0)
        row_bias(2, 1)
        logp_on_scalar(2, 1)
        fetch(0, 1)
        fetch(1, 0)
        logp_from_copy(1, 1, nc.vector)
        fetch(1, 1)
        fetch(2, 0)
        fetch(2, 1, pieces=2)
